import numpy as np, ml_dtypes
CORES = [5,29,101,125,133,157,229,253]
N = 8
BF = ml_dtypes.bfloat16
def gentries(a):
    return np.ascontiguousarray(a.reshape(8, 16, -1).transpose(0, 2, 1)).reshape(8, -1)
def gtable(e):
    e = np.asarray(e); return np.ascontiguousarray(e.reshape(8, -1, 16).transpose(0, 2, 1)).reshape(128, -1).astype(np.int32)
VA, G, OB, W, CAP, S = 640, 384, 1280, 2560, 240, 176
E0, M, RO = 3, 14, 5
WA, NIL = VA + G, W - 1
H = NIL - OB
KC = 6
def within(rng, ke, k):
    o = np.argsort(ke, kind="stable"); cnt = np.bincount(ke, minlength=KC); lo = np.add.accumulate(cnt) - cnt
    i = lo[k] + (rng.random(k.shape) * np.maximum(cnt[k], 1)).astype(np.int64)
    return o[np.minimum(i, ke.size - 1)]
def feat(rng, cen, k, a):
    v = np.swapaxes(cen[np.arange(8)[None, :, None], k], 2, 3)
    return v + rng.integers(-a, a + 1, v.shape)
def parts(rng, bd=None):
    if bd is None: bd = np.argsort(rng.random((N, 8, VA)), axis=-1)[..., :G]
    cen = rng.integers(-90, 91, (8, KC, 16)); ka = rng.integers(0, KC, (N, 8, VA)); kb = rng.integers(0, KC, (N, 8, OB))
    kx = np.concatenate([ka, np.take_along_axis(np.roll(ka, 1, axis=0), np.roll(bd, 1, axis=0), 2)], axis=2)
    eo = np.argsort(kx[:, :, None, :] + 1.5 * rng.random((N, 8, 16, WA)), axis=-1); ao = np.argsort(ka[:, :, None, :] + 1.5 * rng.random((N, 8, 16, VA)), axis=-1)
    nba = np.empty((N, 8, 16, VA), np.int64); np.put_along_axis(nba, ao, eo[..., np.arange(VA) * WA // VA], -1)
    ky = np.concatenate([kb, np.roll(kb, -1, axis=0)[..., :H]], axis=2); nbb = np.empty((N, 8, 16, OB), np.int64); f0 = np.empty((N, 8, 16, S), np.int64)
    dens = rng.choice(np.array([0.3, 0.5, 0.8]), (N, 8))
    for r in range(N):
        for g in range(8):
            k = np.where(rng.random((16, OB)) < 0.75, kb[r, g], rng.integers(0, KC, (16, OB)))
            nbb[r, g] = np.where(rng.random((16, OB)) < 0.04, NIL, within(rng, ky[r, g], k))
            keep = (rng.random((16, S)) < dens[r, g]) & (rng.random((1, S)) > 0.1)
            f0[r, g] = np.where(keep, within(rng, ky[r, g], np.broadcast_to(ka[r, g, :S], (16, S))), NIL)
    return dict(cen=cen, ka=ka, kb=kb, bd=bd, nba=nba, nbb=nbb, f0=f0, xa=feat(rng, cen, ka, 3), xb=feat(rng, cen, kb, 3))
def pack(d):
    t = lambda v, w: np.ascontiguousarray(np.reshape(v, (N, 128, w)))
    return {"xa": t(d["xa"], VA).astype(np.float32).astype(BF), "xb": t(d["xb"], OB).astype(np.float32).astype(BF), "nba": t(d["nba"], VA).astype(np.int32),
            "nbb": t(d["nbb"], OB).astype(np.int32), "f0": t(d["f0"], S).astype(np.int32), "bd": np.stack([gtable(a) for a in d["bd"]])}
def put(row, c, v):
    o = np.setdiff1d(np.arange(row.size), c); hit = o[np.isin(row[o], v)]
    row[hit] = np.setdiff1d(row[c], v)[:hit.size]; row[c] = v
def short(rng, d, r, g):
    z1, z2, x = S, S + 1, VA - 1; P = np.array([S // 4, S // 2, 3 * S // 4, VA - 4, VA - 3, VA - 2])
    T = rng.permutation(np.setdiff1d(np.arange(S), P[:3])); D1, D2 = int(T[0]), int(T[1]); T = T[2:]
    f = d["f0"][r, g]; f[:] = rng.integers(0, NIL, f.shape); f[:, P[:3]] = NIL; f[:15, D1] = NIL; f[:15, D2] = NIL
    m = np.concatenate([P[:3], np.arange(S + 2, VA)])
    for p in range(16):
        c, v = [z1, z2], [D1, D2]
        if p == 0: c, v = [z1, z2, x], [x, z1, int(T[0])]
        elif p == 1: v = [z2, D2]
        elif p == 2: c, v = [z1, z2, x], [D1, D2, z1]
        elif p < 9: c, v = [z1, z2, int(P[p - 3])], [D1, D2, z2]
        elif p < 15:
            i = m[(p - 9) * T.size:(p - 8) * T.size]; c, v = np.concatenate([c, i]), np.concatenate([v, T[:i.size]])
        else: v = [z1, z2]
        put(d["nba"][r, g, p], np.array(c, np.int64), np.array(v, np.int64))
def lone(rng, d, r, g, z0, L):
    c, u, w = OB - 1, VA - 1, S
    f = d["f0"][r, g]; nb = d["nba"][r, g]; v = rng.integers(0, NIL - 1, S)
    f[:] = NIL; f[rng.integers(0, 16, S), np.arange(S)] = v + (v >= c); f[:, 64 + rng.permutation(S - 64)[:z0]] = NIL
    f[:, 0] = NIL; f[0, 0] = NIL - 1; f[1:3, 1] = c
    cells = [0, u, w] if L == 0 else [u, u - 1] + [S + i for i in range(L)]
    d["xa"][r, g][:, cells] = 40; d["xb"][r, g][:, c] = 40; d["nbb"][r, g][:, c] = c
    for p in range(16):
        if L == 0:
            to = {u: p}
            if p == 1: to[w] = u
            if p == 2: to[0] = 1
            if p == 3: to[0] = w
        else:
            to = {u: 1 if p == 1 else S, u - 1: S if p == 1 else (1 if p == 2 else p)}
            for i in range(1, L + 1): to[S + i - 1] = u if p == 4 + i else (S + i if p == 3 and i < L else 16 * i + p)
        k = sorted(to); put(nb[p], np.array(k, np.int64), np.array([to[i] for i in k], np.int64))
def quiet(rng, d, r):
    for g in range(8):
        o = rng.permutation(min(S, CAP)); x, y = int(o[0]), int(o[1]); z = int(rng.integers(2 * CAP + 1, VA)); c = int(rng.integers(0, OB))
        d["f0"][r, g] = NIL; d["f0"][r, g][:, y] = c
        for p in range(16):
            d["nba"][r, g, p] = rng.permutation(VA)
            if p == 0: k, v = [x, y], [y, x]
            else: k, v = [x, z, y], [x, y, z]
            put(d["nba"][r, g, p], np.array(k, np.int64), np.array(v, np.int64))
        b = d["xb"][r, g][:, c]; d["xa"][r, g][:, x] = b + (E0 if g < 7 else E0 + 1); d["xa"][r, g][:, z] = b - (E0 + 1)
def setup_inputs(rng):
    return pack(parts(rng))
def setup_inputs_room(rng):
    d = parts(rng); d["xa"] = feat(rng, d["cen"], d["ka"], 1); d["xb"] = feat(rng, d["cen"], d["kb"], 1); z0 = (S - VA) % CAP
    d["xa"][:, ::2, M - 1:] = 127; d["xb"][:, ::2, M - 1:] = -127; d["xa"][:, 1::2, M:] = 127; d["xb"][:, 1::2, M:] = -127
    d["xa"][:, 1::4, :M] = rng.integers(-1, 2, (N, 2, M, VA)); d["xb"][:, 1::4, :M] = rng.integers(-1, 2, (N, 2, M, OB))
    for r in range(N):
        for g in (0, 4):
            z = z0 + (0, 1, -1)[(r + g // 2) % 3]; o = rng.permutation(S)
            d["f0"][r, g][:, o[:z]] = NIL; d["f0"][r, g, rng.integers(0, 16, S - z), o[z:]] = rng.integers(0, NIL, S - z)
        lone(rng, d, r, 2, z0, 0); lone(rng, d, r, 6, z0, RO - (VA - S + z0) // CAP)
        for g in (1, 5): short(rng, d, r, g)
    return pack(d)
def setup_inputs_ties(rng):
    d = parts(rng); d["xb"] = feat(rng, d["cen"], d["kb"], 0); v = feat(rng, d["cen"], d["ka"], 0)
    d["xa"] = v + rng.choice(np.array([0, E0, E0 + 1, E0 + 2]), v.shape, p=[0.3, 0.55, 0.12, 0.03]) * rng.choice(np.array([-1, 1]), v.shape)
    d["f0"][:, ::2] = d["f0"][:, ::2, :1].copy(); d["nbb"][:, 1::2] = d["nbb"][:, 1::2, 5:6].copy(); d["nbb"][:, 0, 15] = np.arange(OB)
    quiet(rng, d, 0)
    return pack(d)
def setup_inputs_ends(rng):
    o = 1 + np.argsort(rng.random((N, 8, VA - 2)), axis=-1)[..., :G - 2]; z = np.zeros((N, 8, 1), np.int64)
    d = parts(rng, np.concatenate([z, o, z + VA - 1], axis=2)); ends = np.array([0, H - 1, H, OB - 1, OB, W - 2, NIL])
    d["cen"][::2] = d["cen"][::2, :1].copy(); d["cen"][4] = 125; d["cen"][6] = -125
    d["xa"] = feat(rng, d["cen"], d["ka"], 2); d["xb"] = feat(rng, d["cen"], d["kb"], 2)
    d["f0"] = np.where(rng.random(d["f0"].shape) < 0.5, rng.choice(ends, d["f0"].shape), d["f0"])
    e = d["nbb"][:, ::2]; d["nbb"][:, ::2] = np.where(rng.random(e.shape) < 0.5, rng.choice(ends, e.shape), e)
    d["nbb"][:, 5] = NIL; d["f0"][0, 7] = NIL; d["nba"][:, 2, 0] = np.arange(VA); d["nba"][:, 2, 1] = WA - 1 - np.arange(VA)
    return pack(d)
def setup_inputs_cross(rng):
    h = min(S, G) // 2; a = np.argsort(rng.random((N, 8, S)), axis=-1)[..., :h]; b = S + np.argsort(rng.random((N, 8, VA - S)), axis=-1)[..., :G - h]
    bd = np.concatenate([a, b], axis=2); bd = np.take_along_axis(bd, np.argsort(rng.random(bd.shape), axis=-1), 2); d = parts(rng, bd)
    noise = np.full((1, 8, 1, 1), 3); noise[:, :2] = 1; d["xa"] = feat(rng, d["cen"], d["ka"], noise); d["xb"] = feat(rng, d["cen"], d["kb"], noise)
    for r in range(N):
        for g in range(8):
            far = OB + within(rng, d["kb"][(r + 1) % N, g, :H], np.broadcast_to(d["ka"][r, g, :S], (16, S))); f = d["f0"][r, g]
            d["f0"][r, g] = np.where((f != NIL) & (rng.random(f.shape) < 0.8), far, f)
    d["f0"][1::2, :4] = NIL; lo = np.arange(VA) < CAP
    for r in range(1, N, 2):
        for g in (0, 1):
            for p in range(16):
                row = d["nba"][r, g, p]; gh = row >= VA
                i = np.flatnonzero(gh & (lo == (g == 0))); j = np.flatnonzero(~gh & (lo == (g == 1))); k = min(i.size, j.size); i = i[:k]; j = j[:k]
                vi = row[i].copy(); row[i] = row[j]; row[j] = vi
    return pack(d)
def setup_inputs_spread(rng):
    d = parts(rng); cen = rng.integers(-127, 128, (8, KC, 16))
    for x, k, n in (("xa", d["ka"], VA), ("xb", d["kb"], OB)):
        v = np.clip(feat(rng, cen, k, rng.choice(np.array([0, 1, 2, 2, 3, 3, 5, 12]), (N, 8, 1, n))), -127, 127)
        v = np.where(rng.random((N, 8, 1, n)) < 0.125, rng.integers(-127, 128, v.shape), v)
        d[x] = v * (rng.random((N, 8, 1, n)) > 0.0625)
    d["nba"][:, :, 4:8] = np.argsort(rng.random((N, 8, 4, WA)), axis=-1)[..., :VA]
    d["nbb"] = np.where(rng.random(d["nbb"].shape) < 0.3, rng.integers(0, W, d["nbb"].shape), d["nbb"])
    return pack(d)
def check_inputs(d):
    bad = []
    for k, hi in (("nba", WA - 1), ("nbb", NIL), ("f0", NIL), ("bd", VA - 1)):
        if np.min(d[k]) < 0 or np.max(d[k]) > hi: bad.append("range of " + k)
    for k in ("xa", "xb"):
        v = d[k].astype(np.float32)
        if not np.all((v >= -127) & (v <= 127) & (np.rint(v) == v)): bad.append("whole numbers of " + k)
    s = np.sort(d["nba"], axis=2)
    if np.any(s[..., 1:] == s[..., :-1]): bad.append("repeated in a row of nba")
    s = np.sort(np.stack([gentries(a) for a in d["bd"]]), axis=2)
    if np.any(s[..., 1:] == s[..., :-1]): bad.append("repeated in bd")
    return bad
def reference(xa, xb, nba, nbb, f0, bd):
    A = xa.astype(np.float32).astype(np.int32).reshape(N, 8, 16, VA); own = xb.astype(np.float32).astype(np.int32).reshape(N, 8, 16, OB)
    na = nba.astype(np.int64).reshape(N, 8, 16, VA); no = nbb.astype(np.int64).reshape(N, 8, 16, OB); bl = np.stack([gentries(a) for a in bd]).astype(np.int64)
    B = np.zeros((N, 8, 16, W), np.int32); NB = np.full((N, 8, 16, W), NIL, np.int64)
    for r in range(N):
        q = (r + 1) % N; n = no[q, :, :, :H]
        B[r, :, :, :OB] = own[r]; B[r, :, :, OB:NIL] = own[q, :, :, :H]
        NB[r, :, :, :OB] = no[r]; NB[r, :, :, OB:NIL] = np.where(n < H, OB + n, NIL)
    F = np.full((N, 8, 16, VA), NIL, np.int64); F[..., :S] = f0.reshape(N, 8, 16, S)
    flag = np.ones((N, 8, VA), bool); e = [E0] * N; rows = np.arange(16)[:, None]
    for wave in range(RO):
        ext = []
        for r in range(N):
            q = (r - 1) % N; n = np.take_along_axis(F[q], bl[q][:, None, :], 2)
            ext.append(np.concatenate([F[r], np.where((n >= OB) & (n < NIL), n - OB, NIL)], axis=2))
        for r in range(N):
            good = 0
            for g in range(8):
                a = np.flatnonzero(flag[r, g] & np.all(F[r, g] == NIL, axis=0))[:CAP]
                x = A[r, g][:, a]; c = ext[r][g][rows, na[r, g][:, a]]; col = np.arange(a.size)
                new = np.full(c.shape, NIL, np.int64)
                for t in range(3):
                    near = (np.abs(B[r, g][:, c] - x[:, None, :]) <= e[r]).astype(np.int32)
                    v = (c != NIL) & (np.add.reduce(near, axis=0) >= M); new = np.where(v, c, new); some = np.any(v, axis=0)
                    if t == 0:
                        ok = some; b = np.where(ok, c[np.argmax(v, axis=0), col], NIL)
                    else:
                        b = np.where(some, c[15 - np.argmax(v[::-1], axis=0), col], b)
                    c = NB[r, g][:, b]
                s = a[ok]; b = b[ok]; F[r, g][:, s] = new[:, ok]
                A[r, g][:, s] = x[:, ok] + np.clip(B[r, g][:, b] - x[:, ok], -2, 2)
                flag[r, g, a] = False
                w = na[r, g][:, s].reshape(-1); flag[r, g, w[w < VA]] = True
                good += int(s.size)
            e[r] = E0 + (good & 1)
    return {"yf": F.reshape(N, 128, VA).astype(np.float32), "ya": A.reshape(N, 128, VA).astype(np.float32).astype(BF)}

@@ -1,0 +1,525 @@
+from concourse.mybir import AluOpType as O, ActivationFunctionType as F
+
+VA, GH, OB, CAP, S0, RO = 640, 384, 1280, 240, 176, 5
+OFF, NULLC, ZC = 9, 2568, 1288
+EXT = OFF + OB
+WB = 2576
+WE = 1264
+NB_HALF = 640
+CH = ((0, 96), (96, 64), (160, 80))
+S_ACT = ()
+
+SCRATCH = {}
+_L = {
+    "bfloat16": "ZB:2576 XA:1264 EM:1264 FLB:640 MB:176 ONB:128 BD:128 BDT:128 ID:128 SLM:128 SUM:128 LU:128 FU:128 IDH:128 IDB:128 "
+                "SLN:128 TRIX:128 BDN:128 GS:2048 EB:2048 HB:512 DJ:240 ON80:96 EL:40 XD:240 XC:240 SC:240 XM:240 XN:240 RX:640 "
+                "XR0:3840 XR1:3840 XF0:240 XF1:240 NO0:240 NO1:240 D:3840 SQ:3840 NR:3840 SG:240",
+    "float16": "LWH:240 GW:2048 EH:2048 HS:512 NEGS:96 TT:256 TTT:256 NFH0:240 NFH1:240 ST:3840 T2:240 SP:720",
+    "float32": "NB:2576 FX:1264 FL:1264 LW:1280 MF:176 FA:176 EF:2048 O16:128 COL:8 JR:240 "
+               "DUMROW:240 IOTAF:640 DUMA0:40 DUMPA:40 C20:240 ZROW:240 ONE40:40 CUM:40 PO1:40 PO2:40 THR:8 NFAIL:16 "
+               "YM:640 Y1:640 YO:640 SF:3840 Z:240 OK:240 NW:240 NX:240",
+    "int32": "NBB:1280 NBA:1264 F0I:176 BDI:24 ICOL:4 KI:240 NI:240",
+    "uint16": "NBX:1280 LN:1280 BDU:24 POU:40 FT:256 BW2:16 RN:640 GHS:1920 RG:1920 LG:1920 NFU0:240 NFU1:240 AW0:16 AW1:16 "
+              "LU0:240 LU1:240 OFS:240 OBW:24",
+}
+for _d in _L:
+    for _x in _L[_d].split():
+        SCRATCH[_x.split(":")[0]] = ("sbuf", [128, int(_x.split(":")[1])], _d)
+for _i in range(8):
+    SCRATCH["ps%d" % _i] = ("psum", [128, 512], "float32")
+
+LOADS = ["xb", "f0", "bd", "nba", "xa", "nbb"]
+SEMAPHORES = ["sV", "sA", "sP", "sG", "ls", "oy", "ox", "rx", "rn", "ax0", "ax1", "an0", "an1"] + \
+    ["l" + n for n in LOADS] + ["rg%d" % w for w in range(RO)] + ["ag%d" % w for w in range(RO)]
+
+
+def relays(topo, src, dst):
+    c = [x for x in topo.cores_of(src) if x != src and topo.may_write(x, dst)]
+    return sorted(c, key=lambda x: (topo.die(x) != topo.die(src), x))
+
+
+def messages(topo, cores):
+    n, out = len(cores), []
+    for r in range(n):
+        src, prev, nxt = cores[r], cores[(r - 1) % n], cores[(r + 1) % n]
+        rb = relays(topo, src, prev)
+        w = (NB_HALF, OB - 1 - NB_HALF)
+        for i in range(2):
+            a, b = i * NB_HALF, i * NB_HALF + w[i]
+            out.append((src, rb[i], prev, "RX", (0, w[i]), "rx", "ZB", (EXT + a, EXT + b), "ax%d" % i, "ZB", (OFF + a, OFF + b)))
+        for i in range(2):
+            a, b = i * NB_HALF, i * NB_HALF + w[i]
+            out.append((src, rb[2 + i], prev, "RN", (0, w[i]), "rn", "LN", (a, b), "an%d" % i, "NBX", (a, b)))
+        rg = relays(topo, src, nxt)
+        for k in range(RO):
+            s = (k * GH, (k + 1) * GH)
+            out.append((src, rg[0], nxt, "RG", s, "rg%d" % k, "LG", s, "ag%d" % k, "GHS", s))
+    return out
+
+
+def send(g, topo, src, dst, dbuf, dcol, sbuf, scol, T, rsem):
+    rid, pid = topo.addr(dst, src)
+    g.remote_dma(T[dbuf][:, dcol[0]:dcol[1]], T[sbuf][:, scol[0]:scol[1]], T.sem[rsem], T.sem["ls"], pid, rid, topo.mask(src, dst))
+    return len(topo.engines(src, dst))
+
+
+def relay_program(g, core, T, topo, msgs):
+    total = 0
+    for m in msgs:
+        if m[1] == core:
+            g.wait_ge(T.sem[m[5]], len(topo.engines(m[0], core)))
+            total += send(g, topo, core, m[2], m[6], m[7], m[3], m[4], T, m[8])
+    if total:
+        g.wait_ge(T.sem["ls"], total)
+
+
+CY = 0.00083 * 1.25
+GA, SCA = 1.5, 3.6
+
+
+def build(g, core, T, topo, msgs):
+    tasks, lastw, readers = [], {}, {}
+    V, A, P, SY = g.vector, g.scalar, g.tensor, g.sync
+    COL = {x: T.COL[:, i:i + 1] for i, x in enumerate(("PF", "BIASL", "BIASF", "M0", "M1", "C0", "C2", "C02"))}
+    ICOL = {x: T.ICOL[:, i:i + 1] for i, x in enumerate(("PI", "PJ", "EI", "EJ"))}
+
+    def tk(q, dur, rd, wr, fn, sem=None, val=0):
+        deps = {}
+        i = len(tasks)
+        for b in rd:
+            if b in lastw:
+                deps[lastw[b]] = True
+        for b in wr:
+            if b in lastw:
+                deps[lastw[b]] = True
+            for x in readers.get(b, []):
+                deps.setdefault(x, False)
+        for b in rd:
+            if b not in wr:
+                readers.setdefault(b, []).append(i)
+        for b in wr:
+            lastw[b] = i
+            readers[b] = []
+        tasks.append(dict(q=q, dur=dur, deps=deps, fn=fn, sem=sem, val=val))
+
+    def cost(n, c):
+        return 0.06 + max(64, n * c) * CY
+
+    def vts(out, in0, s1, s2, o0, o1, rd, wr, n, c=1.0):
+        if o1 is None:
+            tk("V", cost(n, c), rd, wr, lambda: V.tensor_scalar(out, in0, s1, None, op0=o0))
+        else:
+            tk("V", cost(n, c), rd, wr, lambda: V.tensor_scalar(out, in0, s1, s2, op0=o0, op1=o1))
+
+    def vtt(out, a, b, op, rd, wr, n, c=2.0):
+        tk("V", cost(n, c), rd, wr, lambda: V.tensor_tensor(out, a, b, op))
+
+    def vcp(out, in_, rd, wr, n, c=1.0):
+        tk("V", cost(n, c), rd, wr, lambda: V.tensor_copy(out, in_))
+
+    def vms(ap, x, wr, n, c=1.0):
+        tk("V", cost(n, c), [], wr, lambda: V.memset(ap, x))
+
+    def act(out, in_, fn, rd, wr, n, c=1.0, **kw):
+        tk("A", 0.07 + n * c * CY, rd, wr, lambda: A.activation(out, in_, fn, **kw))
+
+    def mm(lst, rd, wr, cyc):
+        def fn():
+            x = None
+            for o, l, r, a, b in lst:
+                x = P.matmul(o, l, r, a, b)
+            return x
+        tk("P", 0.05 + cyc * 0.00075, rd, wr, fn)
+
+    def iota(out, pat, base, wr, n):
+        tk("G", 0.13 + 2 * n * CY, [], wr, lambda: g.iota(out, pat, base, 0, allow_small_or_imprecise_dtypes=True))
+
+    def asel(out, in_, pat, op, base, cm, rd, wr, n):
+        tk("G", 0.17 + 2 * n * CY, rd, wr, lambda: g.affine_select(out, in_, pat, op, 0.0, base, cm))
+
+    def ch(name, k, w=1):
+        return T[name][:, w * CH[k][0]:w * (CH[k][0] + CH[k][1])]
+
+    def by(name, k, q):
+        return T[name][:, 16 * CH[k][0] + q:16 * (CH[k][0] + CH[k][1]):16]
+
+    def load(q, name, out, wr, rd):
+        e = SY if q == "S" else A
+        tk(q, 0.1, rd, wr, lambda: e.dma_start(out, T[name][:]), sem="l" + name, val=16)
+
+    vms(T.ZB[:, 0:OFF], 1000.0, ["ZBf"], OFF)
+    vms(T.ZB[:, NULLC:WB], 1000.0, ["ZBg"], 8)
+    load("S", "f0", T.F0I[:], ["F0I"], [])
+    load("A", "xb", T.ZB[:, OFF:EXT], ["ZBo"], ["ZBf"])
+    load("S", "bd", T.BDI[:], ["BDI"], [])
+    load("S", "nba", T.NBA[:, 0:VA], ["NBA"], [])
+    load("A", "xa", T.XA[:, 0:VA], ["XA"], [])
+    load("S", "nbb", T.NBB[:], ["NBB"], [])
+
+    mine = [m for m in msgs if m[0] == core]
+    inb = {m[8]: m for m in msgs if m[2] == core}
+    sent = [0]
+
+    def remote(m, rd):
+        def fn():
+            sent[0] += send(g, topo, core, m[1], m[3], m[4], m[9], m[10], T, m[5])
+        tk("G", 0.6, rd, ["snt" + m[8]], fn, sem="none")
+
+    def arrive(sem, wr, delay):
+        m = inb[sem]
+        tk(None, delay, ["snt" + sem], wr, None, sem=sem, val=len(topo.engines(m[1], core)))
+
+    for m in mine[0:2]:
+        remote(m, ["ZBo"])
+
+    vms(T.ONB[:], 1.0, ["ONB"], 128, .5)
+    asel(T.BDT[:], T.ONB[:], [[-16, 8], [0, 16]], O.is_ge, 0, 1, ["ONB"], ["BDT"], 128)
+    asel(T.BD[:], T.BDT[:], [[16, 8], [0, 16]], O.is_ge, 15, -1, ["BDT"], ["BD"], 128)
+    asel(T.ID[:], T.ONB[:], [[-1, 128]], O.is_equal, 0, 1, ["ONB"], ["ID"], 128)
+    tk("G", 0.15, [], ["PI"], lambda: g.iota(ICOL["PI"], [[0, 1]], 0, 1))
+    iota(T.IOTAF[:], [[1, VA]], 0, ["IOTAF"], VA)
+    iota(T.DUMROW[:], [[1, CAP]], 1024, ["DUMROW"], CAP)
+    iota(T.DUMA0[:], [[16, 40]], VA, ["DUMA0"], 40)
+    asel(T.SLM[:], T.BD[:], [[-1, 128]], O.is_gt, 0, 1, ["BD"], ["SLM"], 128)
+    asel(T.SUM[:], T.BD[:], [[1, 128]], O.is_gt, 0, -1, ["BD"], ["SUM"], 128)
+    iota(T.JR[:], [[1, CAP]], 0, ["JR"], CAP)
+
+    vms(T.FX[:, S0:VA], 0.0, ["FX"], VA - S0)
+    vms(T.FX[:, VA + GH:WE], 0.0, ["FX"], CAP)
+    vts(T.MF[:], T.F0I[:], 2559, None, O.is_lt, None, ["F0I"], ["MF"], S0)
+    vts(T.FA[:], T.F0I[:], OFF, None, O.add, None, ["F0I"], ["FA"], S0)
+    vtt(T.FX[:, 0:S0], T.FA[:], T.MF[:], O.mult, ["FA", "MF"], ["FX"], S0)
+    vcp(T.BDU[:], T.BDI[:], ["BDI"], ["BDU"], 24)
+    vcp(T.MB[:], T.MF[:], ["MF"], ["MB"], S0)
+    vms(T.EM[:], 1.0, ["EM"], WE, .5)
+    vms(T.EB[:], 0.0, ["EB"], 2048, .5)
+    EBT, GST, HBT = ["EB"], ["GS"], ["HB"]
+    for q in range(16):
+        act(T.EB[:, 128 * q + q:128 * q + 128:16], T.ID[:, q:128:16], F.Copy, ["ID", "EB"], ["EB%d" % q], 8)
+        EBT.append("EB%d" % q)
+    if S_ACT:
+        act(T.EF[:], T.EB[:], F.Copy, EBT, ["EF"], 2048)
+    vcp(T.EH[:], T.EB[:], EBT, ["EH"], 2048, .5)
+    vms(T.GS[:], 0.0, ["GS"], 2048, .5)
+    for q in range(16):
+        vts(T.GS[:, 128 * q + q:128 * q + 128:16], T.BD[:, q:128:16], 32768.0, None, O.mult, None, ["BD", "GS"], ["GS%d" % q], 8)
+        GST.append("GS%d" % q)
+    vts(T.GW[:], T.GS[:], 1.0 / 32768.0, None, O.mult, None, GST, ["GW"], 2048, .5)
+    vts(ICOL["PJ"], ICOL["PI"], 15, None, O.bitwise_and, None, ["PI"], ["PJ"], 1)
+    vcp(COL["PF"], ICOL["PJ"], ["PJ"], ["PF"], 1)
+    vts(T.DUMPA[:], T.DUMA0[:], COL["PF"], None, O.add, None, ["DUMA0", "PF"], ["DUMPA"], 40)
+    vts(COL["BIASL"], COL["PF"], -14.5, None, O.add, None, ["PF"], ["BIASL"], 1)
+    vts(COL["BIASF"], COL["PF"], -1.0, 0.5, O.mult, O.add, ["PF"], ["BIASF"], 1)
+    vts(COL["M0"], COL["PF"], 0.0, -float(ZC), O.is_equal, O.mult, ["PF"], ["M0"], 1)
+    vts(COL["M1"], COL["PF"], 1.0, None, O.is_equal, None, ["PF"], ["M1"], 1)
+    vts(COL["C0"], COL["PF"], 0.0, 1024.0, O.is_equal, O.mult, ["PF"], ["C0"], 1)
+    vts(COL["C2"], COL["PF"], 2.0, -32768.0, O.is_equal, O.mult, ["PF"], ["C2"], 1)
+    vtt(COL["C02"], COL["C0"], COL["C2"], O.add, ["C0", "C2"], ["C02"], 1)
+    vts(T.DJ[:], T.JR[:], COL["M1"], COL["C02"], O.mult, O.add, ["JR", "M1", "C02"], ["DJ"], CAP)
+    vms(T.ON80[:], 1.0, ["ON80"], 96)
+    vts(T.NEGS[:], T.ON80[:], COL["M0"], None, O.mult, None, ["ON80", "M0"], ["NEGS"], 96)
+    vts(T.IDH[:], T.ID[:], 0.5, None, O.mult, None, ["ID"], ["IDH"], 128, .5)
+    vtt(T.LU[:], T.IDH[:], T.SLM[:], O.subtract, ["IDH", "SLM"], ["LU"], 128)
+    vtt(T.FU[:], T.IDH[:], T.SUM[:], O.subtract, ["IDH", "SUM"], ["FU"], 128)
+    vts(T.IDB[:], T.ID[:], 2048.0, None, O.mult, None, ["ID"], ["IDB"], 128, .5)
+    vts(T.SLN[:], T.SLM[:], -1.0, None, O.mult, None, ["SLM"], ["SLN"], 128, .5)
+    vtt(T.TRIX[:], T.SLN[:], T.IDB[:], O.subtract, ["SLN", "IDB"], ["TRIX"], 128)
+    vts(T.BDN[:], T.BD[:], -2048.0, None, O.mult, None, ["BD"], ["BDN"], 128, .5)
+    vms(T.HB[:], 0.0, ["HB"], 512, .5)
+    for h in range(2):
+        for e in range(2):
+            for a in range(4):
+                c = 128 * (2 * h + e) + 32 * a + 16 * e
+                HBT.append("HB%d" % c)
+                act(T.HB[:, c:c + 16], T.ID[:, 32 * a + 16 * h:32 * a + 16 * h + 16], F.Copy, ["ID", "HB"], [HBT[-1]], 16)
+    vcp(T.HS[:], T.HB[:], HBT, ["HS"], 512, .5)
+    vms(T.O16[:], 1.0 / 16.0, ["O16"], 128)
+    vms(T.ONE40[:], 1.0, ["ONE40"], 40)
+    vms(T.C20[:], 20.0, ["C20"], CAP)
+    vms(T.ZROW[:], 0.0, ["ZROW"], CAP)
+    vms(T.FL[:], 1.0, ["FL"], WE)
+    vms(T.THR[:, 0:1], 9.0, ["THR0"], 1)
+    vms(T.NBA[:, VA:WE], 1024, ["NBAd"], WE - VA)
+    vms(T.XA[:, VA:WE], 0.0, ["XAd"], WE - VA, .5)
+    vms(T.NB[:, 0:OFF], float(NULLC), ["NBf"], OFF)
+    vms(T.NB[:, NULLC:WB], float(NULLC), ["NBg"], 8)
+    vts(T.TT[:, 240:256], T.ONB[:, 0:16], 1024.0, None, O.mult, None, ["ONB"], ["TTp"], 16)
+
+    def ghosts_out(w):
+        vts(T.GHS[:, w * GH:(w + 1) * GH], T.FX[:, 0:VA].indirect(T.BDU[:, 0:24]), float(OB + 8), -float(OB), O.max, O.add,
+            ["FX", "BDU"], ["GHS%d" % w], GH, GA)
+        remote(mine[4 + w], ["GHS%d" % w])
+
+    def ghosts_in(w):
+        arrive("ag%d" % w, ["LG%d" % w], 4.0)
+        vcp(T.FX[:, VA:VA + GH], T.LG[:, w * GH:(w + 1) * GH], ["LG%d" % w], ["FX"], GH)
+
+    ghosts_out(0)
+    vts(T.NBX[:], T.NBB[:], EXT, NULLC, O.add, O.min, ["NBB"], ["NBX"], OB)
+    for m in mine[2:4]:
+        remote(m, ["NBX"])
+    vts(T.NB[:, OFF:EXT], T.NBB[:], OFF, None, O.add, None, ["NBB"], ["NBo"], OB)
+    for i in range(2):
+        arrive("ax%d" % i, ["ZBe%d" % i], 8.0)
+    for i in range(2):
+        arrive("an%d" % i, ["LN%d" % i], 10.0)
+    ZBT = ["ZBf", "ZBg", "ZBo", "ZBe0", "ZBe1"]
+    NBT = ["NBf", "NBg", "NBo", "NBe0", "NBe1"]
+    B = [T["ps%d" % i] for i in range(8)]
+
+    def front(w):
+        p = str(w % 2)
+        el = B[6][:, 0:40]
+        if w == 0:
+            mm([(B[6][:, 40:40 + S0], T.BD[:], T.MB[:], True, True)], ["BD", "MB"], ["ps6"], S0)
+            vts(T.EM[:, 0:S0], B[6][:, 40:40 + S0], 0.0, None, O.is_equal, None, ["ps6"], ["EM", "ps6"], S0)
+        mm([(el, T.EB[:, 128 * q:128 * q + 128], T.EM[:, q:VA:16], q == 0, w == 0 and q == 15) for q in range(16)], ["EM"] + EBT, ["ps6"], 1024)
+        if w:
+            act(T.FLB[:], T.FL[:, 0:VA], F.Copy, ["FL"], ["FLB"], VA)
+            mm([(el, T.EB[:, 128 * q:128 * q + 128], T.FLB[:, q:VA:16], False, q == 15) for q in range(16)], ["FLB"] + EBT, ["ps6"], 1024)
+        vts(T.EL[:], el, 1.5 if w else 0.5, None, O.is_ge, None, ["ps6"], ["EL", "ps6"], 40)
+        mm([(B[6][:, 40:80], T.BD[:], T.EL[:], True, True), (B[6][:, 80:120], T.TRIX[:], T.EL[:], True, True)], ["BD", "TRIX", "EL"], ["ps6"], 128)
+        tk("V", cost(40, 1), ["ONE40"], ["CUM", "ps6"], lambda: V.tensor_tensor_scan(T.CUM[:], T.ONE40[:], B[6][:, 40:80], 2047.0, O.mult, O.add))
+        vtt(T.PO1[:], T.CUM[:], B[6][:, 80:120], O.add, ["CUM"], ["PO1", "ps6"], 40, 1)
+        vtt(T.PO2[:], T.PO1[:], T.DUMPA[:], O.min, ["PO1", "DUMPA"], ["PO2"], 40)
+        vcp(T.POU[:], T.PO2[:], ["PO2"], ["POU"], 40)
+        act(T.LW[:, 0:CAP], T.DUMROW[:], F.Copy, ["DUMROW"], ["LW"], CAP)
+        tk("V", cost(VA, SCA), ["POU", "IOTAF"], ["LW"], lambda: V.tensor_copy(T.LW[:, 0:1280].indirect(T.POU[:, 0:40]), T.IOTAF[:]))
+        vcp(T.LWH[:], T.LW[:, 0:CAP], ["LW"], ["LWH"], CAP)
+        mm([(B[6][:, 120:135], T.EH[:, 128 * q:128 * q + 128], T.LWH[:, q:CAP:16], q == 0, q == 15) for q in range(16)], ["LWH", "EH"], ["ps6"], 1024)
+        vcp(T["LU" + p][:], T.LW[:, 0:CAP], ["LW"], ["LU" + p], CAP)
+        vcp(T["AW" + p][:, 0:15], B[6][:, 120:135], [], ["AW" + p, "ps6"], 15)
+        vcp(T["NFU" + p][:], T.NBA[:, 0:WE].indirect(T["AW" + p][:, 0:15]), ["NBA", "NBAd", "AW" + p], ["NFU" + p], CAP, GA)
+        vcp(T["NFH" + p][:], T["NFU" + p][:], ["NFU" + p], ["NFH" + p], CAP, .5)
+        act(T["XF" + p][:], T.XA[:, 0:WE].indirect(T["AW" + p][:, 0:15]), F.Copy, ["XA", "XAd", "AW" + p], ["XF" + p], CAP, GA)
+        for k in range(3):
+            act(ch("XR" + p, k, 16), T.XA[:, 0:WE].indirect(ch("LU" + p, k)), F.Copy, ["XA", "XAd", "LU" + p], ["XR%s%d" % (p, k)], 16 * CH[k][1], GA)
+        if w < RO - 1:
+            act(T.FL[:, 0:WE].indirect(T["AW" + p][:, 0:15]), T.ZROW[:], F.Tanh, ["ZROW", "AW" + p], ["FL"], CAP, SCA)
+
+    front(0)
+    for i in range(2):
+        a, b = (0, NB_HALF) if i == 0 else (NB_HALF, OB - 1)
+        vcp(T.NB[:, EXT + a:EXT + b], T.LN[:, a:b], ["LN%d" % i], ["NBe%d" % i], b - a)
+
+    def test(w, k, step):
+        p, s, pa, pb = str(w % 2), str(k), "ps%d" % k, "ps%d" % (3 + k)
+        c0, n = CH[k]
+        PA, PB = B[k], B[3 + k]
+        cnt, t1, pick, none = PA[:, 0:n], PB[:, 96:96 + n], PB[:, 192:192 + n], PB[:, 288:288 + n]
+        tk("V", cost(16 * n, GA), ZBT + ["OFS" + s, "XR" + p + s], ["D" + s],
+           lambda: V.tensor_tensor(ch("D", k, 16), T.ZB[:, 0:WB].indirect(ch("OFS", k)), ch("XR" + p, k, 16), O.subtract))
+        act(ch("SQ", k, 16), ch("D", k, 16), F.Square, ["D" + s], ["SQ" + s], 16 * n)
+        vts(ch("NR", k, 16), ch("SQ", k, 16), T.THR[:, w:w + 1], 0.84375, O.is_le, O.subtract, ["SQ" + s, "THR%d" % w], ["NR" + s], 16 * n, .5)
+        mm([(cnt, T.GS[:, 128 * q:128 * q + 128], by("NR", k, q), q == 0, q == 15) for q in range(16)], ["NR" + s] + GST, [pa], 16 * n)
+        act(ch("SG", k), cnt, F.Sign, [], ["SG" + s, pa], n)
+        U = "LU" if step else "FU"
+        mm([(pick, T[U][:], ch("SG", k), True, True), (none, T.BD[:], ch("SG", k), True, True)], [U, "BD", "SG" + s], [pb], 2 * n)
+        act(pick, pick, F.Relu, ["BIASL", "BIASF"], [pb], n, bias=COL["BIASL" if step else "BIASF"])
+        sp = lambda st: T.SP[:, CAP * st + c0:CAP * st + c0 + n]
+        if step == 0:
+            nn, c = ch("NO" + p, k), 4 * (w % 2) + k
+            act(nn, none, F.Relu, [], ["NO" + p + s, pb, "NFAIL%d%d" % (w % 2, k)], n, scale=-0.5, bias=-7.0, accum_out=T.NFAIL[:, c:c + 1])
+            vtt(ch("T2", k), nn, T.NEGS[:, 0:n], O.mult, ["NO" + p + s, "NEGS"], ["T2" + s], n)
+        else:
+            act(none, none, F.Relu, [], [pb], n, scale=-0.5, bias=-7.0)
+            vtt(ch("T2", k), none, sp(step - 1), O.mult, ["SP%s%d" % (s, step - 1)], ["T2" + s, pb], n, 1)
+        vtt(t1, pick, ch("Z", k), O.mult, ["Z" + s], [pb], n, 1)
+        vtt(sp(step), t1, ch("T2", k), O.add, ["T2" + s], ["SP%s%d" % (s, step), pb], n, 1)
+        a, m = CAP * step + c0, n // 16
+        mm([(PB[:, 384:384 + m], T.GW[:, 128 * q:128 * q + 128], T.SP[:, a + q:a + n:16], q == 0, q == 15) for q in range(16)],
+           ["GW", "SP%s%d" % (s, step)], [pb], 1024)
+        if step < 2:
+            vts(T.OBW[:, 8 * k:8 * k + m], PB[:, 384:384 + m], float(ZC), None, O.add, None, [], ["OBW" + s, pb], m)
+        else:
+            vts(T.BW2[:, c0 // 16:c0 // 16 + m], PB[:, 384:384 + m], float(ZC), None, O.add, None, [], ["BW2" + s, pb], m)
+        cand, ct = (ch("Z", k), "Z") if step == 0 else (ch("OK", k), "OK")
+        vtt(cnt, cnt, cand, O.min, [ct + s], [pa], n, 1)
+        if step == 0:
+            vts(ch("NW", k), cnt, -float(ZC), float(ZC), O.max, O.add, [], ["NW" + s, pa], n)
+        elif step == 1:
+            vtt(ch("NX", k), ch("NW", k), cnt, O.max, ["NW" + s], ["NX" + s, pa], n, 1)
+        else:
+            vtt(ch("KI", k), ch("NX", k), cnt, O.max, ["NX" + s], ["KI" + s, pa], n, 1)
+            vts(ch("NI", k), ch("KI", k), 4095, None, O.bitwise_and, None, ["KI" + s], ["NI" + s], n)
+
+    def mark(w, k):
+        p, s = str(w % 2), str(k)
+        c0, n = CH[k]
+        nb = (n + 31) // 32
+        mm([(B[7][:, c0:c0 + n], T.BD[:], ch("DJ", k), True, False), (B[7][:, c0:c0 + n], T.BDN[:], ch("SG", k), False, True)],
+           ["BD", "DJ", "BDN", "SG" + s], ["ps7"], 2 * n)
+        vtt(ch("TT", k), ch("NFH" + p, k), B[7][:, c0:c0 + n], O.max, ["NFH" + p], ["TT" + s, "ps7"], n, 1)
+        tk("V", cost(32 * nb, .5), ["TT" + s, "TTp"], ["TTT" + s], lambda: V.transpose(T.TTT[:, c0:c0 + 32 * nb], T.TT[:, c0:c0 + 32 * nb]))
+        lst = []
+        for q in range(16):
+            for h in range(2):
+                for e in range(2):
+                    i, a = 2 * h + e, 240 + c0 + nb * (2 * q + h)
+                    lst.append((B[7][:, a:a + nb], T.HS[:, 128 * i:128 * i + 128], T.TTT[:, c0 + 16 * e + q:c0 + 32 * nb:32], e == 0, e == 1))
+        mm(lst, ["TTT" + s, "HS"], ["ps7"], 4096)
+        vcp(T.FT[:, c0:c0 + 32 * nb], B[7][:, 240 + c0:240 + c0 + 32 * nb], [], ["FT" + s, "ps7"], 32 * nb)
+        for q in range(16):
+            a = c0 + 2 * nb * q
+            act(T.FL[:, 0:WE].indirect(T.FT[:, a:a + n // 16]), T.C20[:, 0:n], F.Tanh, ["C20", "FT" + s], ["FL"], n, SCA)
+
+    def wave(w):
+        p = str(w % 2)
+        last = w == RO - 1
+        AW15 = T["AW" + p][:, 0:15]
+        ghosts_in(w)
+        for k in range(3):
+            s = str(k)
+            c0, n = CH[k]
+            PA = B[k]
+            off = ch("NFU" + p, k)
+            if k in S_ACT:
+                act(ch("SF", k, 16), T.FX[:, 0:WE].indirect(off), F.Copy, ["FX", "NFU" + p], ["SF" + s], 16 * n, GA, bias=-float(ZC))
+                src, E, cyc = "SF", "EF", 64 * n
+            else:
+                vts(ch("ST", k, 16), T.FX[:, 0:WE].indirect(off), -float(ZC), None, O.add, None, ["FX", "NFU" + p], ["ST" + s], 16 * n, GA)
+                src, E, cyc = "ST", "EH", 16 * n
+            mm([(PA[:, 96:96 + n], T[E][:, 128 * q:128 * q + 128], by(src, k, q), q == 0, q == 15) for q in range(16)], [src + s, E], ["ps%d" % k], cyc)
+            vts(ch("OFS", k), PA[:, 96:96 + n], float(ZC), None, O.add, None, [], ["OFS" + s, "ps%d" % k], n)
+            act(ch("Z", k), PA[:, 96:96 + n], F.Copy, [], ["Z" + s, "ps%d" % k], n)
+            test(w, k, 0)
+            if not last:
+                mark(w, k)
+        if not last:
+            tk("V", cost(CAP, SCA), ["NO%s%d" % (p, k) for k in range(3)] + ["AW" + p], ["EM"],
+               lambda: V.tensor_copy(T.EM[:, 0:WE].indirect(AW15), T["NO" + p][:]))
+            nf = 4 * (w % 2)
+            mm([(B[7][:, 500:501], T.O16[:], T.NFAIL[:, nf + k:nf + k + 1], k == 0, k == 2) for k in range(3)],
+               ["O16"] + ["NFAIL%d%d" % (w % 2, k) for k in range(3)], ["ps7"], 768)
+            vcp(ICOL["EI"], B[7][:, 500:501], [], ["EI", "ps7"], 1)
+            vts(ICOL["EJ"], ICOL["EI"], 1, None, O.bitwise_and, None, ["EI"], ["EJ"], 1)
+            vts(T.THR[:, w + 1:w + 2], ICOL["EJ"], 7.0, 9.0, O.mult, O.add, ["EJ"], ["THR%d" % (w + 1)], 1)
+        for step in (1, 2):
+            up = 4096.0 * step
+            for k in range(3):
+                s, n = str(k), CH[k][1]
+                tk("V", cost(n, GA), NBT + ["OBW" + s], ["OK" + s],
+                   lambda k=k, n=n, up=up: V.tensor_scalar(ch("OK", k), T.NB[:, 0:WB].indirect(T.OBW[:, 8 * k:8 * k + n // 16]), up, None, op0=O.add))
+                vts(ch("OFS", k), ch("OK", k), -up, None, O.add, None, ["OK" + s], ["OFS" + s], n)
+                act(ch("Z", k), ch("OK", k), F.Copy, ["OK" + s], ["Z" + s], n, bias=-up - ZC)
+                test(w, k, step)
+        for k in range(3):
+            c0, n = CH[k]
+            tk("V", cost(n, SCA), ["NI%d" % k, "AW" + p], ["FX"],
+               lambda k=k, c0=c0, n=n: V.tensor_copy(T.FX[:, 0:WE].indirect(T["AW" + p][:, c0 // 16:(c0 + n) // 16]), ch("NI", k)))
+        if not last:
+            ghosts_out(w + 1)
+            front(w + 1)
+        XFP = T["XF" + p][:]
+        tk("V", cost(CAP, GA), ZBT + ["BW2%d" % k for k in range(3)] + ["XF" + p], ["XD"],
+           lambda: V.tensor_tensor(T.XD[:], T.ZB[:, 0:WB].indirect(T.BW2[:, 0:15]), XFP, O.subtract))
+        vts(T.XC[:], T.XD[:], -2.0, 2.0, O.max, O.min, ["XD"], ["XC"], CAP, .5)
+        act(T.SC[:], T["NO" + p][:], F.Copy, ["NO%s%d" % (p, k) for k in range(3)], ["SC"], CAP, scale=-1.0, bias=1.0)
+        vtt(T.XM[:], T.XC[:], T.SC[:], O.mult, ["XC", "SC"], ["XM"], CAP)
+        vtt(T.XN[:], T.XM[:], XFP, O.add, ["XM", "XF" + p], ["XN"], CAP)
+        tk("V", cost(CAP, SCA), ["XN", "AW" + p], ["XA"], lambda: V.tensor_copy(T.XA[:, 0:WE].indirect(AW15), T.XN[:]))
+
+    for w in range(RO):
+        wave(w)
+    vts(T.YM[:], T.FX[:, 0:VA], 0.0, 2559.0 + OFF, O.is_equal, O.mult, ["FX"], ["YM"], VA)
+    act(T.Y1[:], T.FX[:, 0:VA], F.Copy, ["FX"], ["Y1"], VA, bias=-float(OFF))
+    vtt(T.YO[:], T.Y1[:], T.YM[:], O.add, ["Y1", "YM"], ["YO"], VA)
+    tk("S", 0.1, ["YO"], ["yf"], lambda: SY.dma_start(T.yf[:], T.YO[:]), sem="oy", val=16)
+    tk("S", 0.1, ["XA"], ["ya"], lambda: SY.dma_start(T.ya[:], T.XA[:, 0:VA]), sem="ox", val=16)
+    return tasks, sent
+
+
+LAT = {"V": 0.05, "A": 0.08, "P": 0.1, "G": 0.1, None: 0.0}
+
+
+def plan(tasks):
+    n = len(tasks)
+    succ = [[] for _ in range(n)]
+    for i, t in enumerate(tasks):
+        for d in t["deps"]:
+            succ[d].append(i)
+    lat = [LAT[t["q"]] if t["sem"] is None or t["q"] is None else 2.2 for t in tasks]
+    prio = [0.0] * n
+    for i in range(n - 1, -1, -1):
+        prio[i] = tasks[i]["dur"] + lat[i] + max([prio[j] for j in succ[i]] + [0.0])
+    left = [len(t["deps"]) for t in tasks]
+    est, fin, free, order = [0.0] * n, [0.0] * n, {}, []
+    ready = {}
+    for i in range(n):
+        if left[i] == 0:
+            ready.setdefault(tasks[i]["q"], []).append(i)
+    while len(order) < n:
+        best = None
+        for q, lst in ready.items():
+            if not lst:
+                continue
+            f = free.get(q, 0.0) if q is not None else 0.0
+            t0 = min(max(f, est[i]) for i in lst)
+            c = max((i for i in lst if max(f, est[i]) <= t0 + 0.06), key=lambda i: prio[i])
+            if best is None or t0 < best[0]:
+                best = (t0, q, c)
+        t0, q, i = best
+        ready[q].remove(i)
+        fin[i] = (est[i] if q is None else max(t0, est[i])) + tasks[i]["dur"]
+        if q is not None:
+            free[q] = fin[i]
+        order.append(i)
+        for j in succ[i]:
+            est[j] = max(est[j], fin[i] + lat[i])
+            left[j] -= 1
+            if left[j] == 0:
+                ready.setdefault(tasks[j]["q"], []).append(j)
+    return order, fin
+
+
+def emit(g, T, tasks, order):
+    queues = {"V": g.vector, "A": g.scalar, "P": g.tensor, "G": g, "S": g.sync}
+    esem = {"V": "sV", "A": "sA", "P": "sP", "G": "sG"}
+    cnt = {k: 0 for k in esem}
+    known = {k: {} for k in queues}
+    done, clock, final = [None] * len(tasks), [None] * len(tasks), {}
+    for i in order:
+        t = tasks[i]
+        q = t["q"]
+        if q is None:
+            done[i] = (t["sem"], t["val"])
+            clock[i] = {t["sem"]: t["val"]}
+            final[t["sem"]] = t["val"]
+            continue
+        kn = known[q]
+        need = [d for d, hard in t["deps"].items() if done[d] is not None and (hard or tasks[d]["q"] != q or tasks[d]["sem"] is not None)]
+        need.sort(key=lambda d: -done[d][1])
+        for d in need:
+            s, v = done[d]
+            if kn.get(s, 0) < v:
+                queues[q].wait_ge(T.sem[s], v)
+            for a, b in clock[d].items():
+                if kn.get(a, 0) < b:
+                    kn[a] = b
+        x = t["fn"]()
+        if t["sem"] == "none":
+            continue
+        if t["sem"] is not None:
+            x.then_inc(T.sem[t["sem"]], 16)
+            done[i] = (t["sem"], 16)
+        else:
+            cnt[q] += 1
+            x.then_inc(T.sem[esem[q]], 1)
+            done[i] = (esem[q], cnt[q])
+        clock[i] = dict(kn)
+        clock[i][done[i][0]] = done[i][1]
+        final[done[i][0]] = max(final.get(done[i][0], 0), done[i][1])
+    return final
+
+
+def rank_program(g, core, T, topo):
+    msgs = messages(topo, T.cores)
+    if T.rank_of(core) is None:
+        relay_program(g, core, T, topo, msgs)
+        return
+    tasks, sent = build(g, core, T, topo, msgs)
+    order, _fin = plan(tasks)
+    final = emit(g, T, tasks, order)
+    for s, v in final.items():
+        g.wait_ge(T.sem[s], v)
+    g.wait_ge(T.sem["ls"], sent[0])

@@ -7,25 +7,25 @@ WB = 2576
 WE = 1264
 NB_HALF = 640
 CH = ((0, 96), (96, 64), (160, 80))
-S_ACT = ()
+S_ACT = (1,)
 
 SCRATCH = {}
 _L = {
     "bfloat16": "ZB:2576 XA:1264 EM:1264 FLB:640 MB:176 ONB:128 BD:128 BDT:128 ID:128 SLM:128 SUM:128 LU:128 FU:128 IDH:128 IDB:128 "
-                "SLN:128 TRIX:128 BDN:128 GS:2048 EB:2048 HB:512 DJ:240 ON80:96 EL:40 XD:240 XC:240 SC:240 XM:240 XN:240 RX:640 "
-                "XR0:3840 XR1:3840 XF0:240 XF1:240 NO0:240 NO1:240 D:3840 SQ:3840 NR:3840 SG:240",
-    "float16": "LWH:240 GW:2048 EH:2048 HS:512 NEGS:96 TT:256 TTT:256 NFH0:240 NFH1:240 ST:3840 T2:240 SP:720",
-    "float32": "NB:2576 FX:1264 FL:1264 LW:1280 MF:176 FA:176 EF:2048 O16:128 COL:8 JR:240 "
+                "SLN:128 TRIX:128 BDN:128 BDM:128 GS:2048 EB:2048 HB:512 DJ:240 EL:40 XD:240 XC:240 XN:240 RX:640 "
+                "XR0:3840 XR1:3840 XF0:240 XF1:240 NO0:240 NO1:240 D:3840 SQ:3840 NR:3840 SG:240 NN:240",
+    "float16": "LWH:240 BDH:128 SELH:8 Y:384 EH:2048 HS:512 TT:256 TTT:256 NFH0:240 NFH1:240 ST:3840 SP:240",
+    "float32": "NB:2576 FX:1264 FL:1264 LW:1280 MF:176 FA:176 EF:2048 O16:128 COL:8 JR:240 MQ:128 MASK:128 BF:48 BM:48 BS:16 "
                "DUMROW:240 IOTAF:640 DUMA0:40 DUMPA:40 C20:240 ZROW:240 ONE40:40 CUM:40 PO1:40 PO2:40 THR:8 NFAIL:16 "
                "YM:640 Y1:640 YO:640 SF:3840 Z:240 OK:240 NW:240 NX:240",
     "int32": "NBB:1280 NBA:1264 F0I:176 BDI:24 ICOL:4 KI:240 NI:240",
     "uint16": "NBX:1280 LN:1280 BDU:24 POU:40 FT:256 BW2:16 RN:640 GHS:1920 RG:1920 LG:1920 NFU0:240 NFU1:240 AW0:16 AW1:16 "
-              "LU0:240 LU1:240 OFS:240 OBW:24",
+              "LU0:240 LU1:240 OFS:240 OBW:48",
 }
 for _d in _L:
     for _x in _L[_d].split():
         SCRATCH[_x.split(":")[0]] = ("sbuf", [128, int(_x.split(":")[1])], _d)
-for _i in range(8):
+for _i in range(7):
     SCRATCH["ps%d" % _i] = ("psum", [128, 512], "float32")
 
 LOADS = ["xb", "f0", "bd", "nba", "xa", "nbb"]
@@ -100,7 +100,8 @@ def build(g, core, T, topo, msgs):
         for b in wr:
             lastw[b] = i
             readers[b] = []
-        tasks.append(dict(q=q, dur=dur, deps=deps, fn=fn, sem=sem, val=val))
+        tag = "".join(x for x in wr[0] if x.isalpha()) + (q or "")
+        tasks.append(dict(q=q, dur=dur, deps=deps, fn=fn, sem=sem, val=val, tag=tag))
 
     def cost(n, c):
         return 0.06 + max(64, n * c) * CY
@@ -131,8 +132,8 @@ def build(g, core, T, topo, msgs):
             return x
         tk("P", 0.05 + cyc * 0.00075, rd, wr, fn)
 
-    def iota(out, pat, base, wr, n):
-        tk("G", 0.13 + 2 * n * CY, [], wr, lambda: g.iota(out, pat, base, 0, allow_small_or_imprecise_dtypes=True))
+    def iota(out, pat, base, wr, n, rd=()):
+        tk("G", 0.13 + 2 * n * CY, list(rd), wr, lambda: g.iota(out, pat, base, 0, allow_small_or_imprecise_dtypes=True))
 
     def asel(out, in_, pat, op, base, cm, rd, wr, n):
         tk("G", 0.17 + 2 * n * CY, rd, wr, lambda: g.affine_select(out, in_, pat, op, 0.0, base, cm))
@@ -177,12 +178,17 @@ def build(g, core, T, topo, msgs):
     asel(T.BD[:], T.BDT[:], [[16, 8], [0, 16]], O.is_ge, 15, -1, ["BDT"], ["BD"], 128)
     asel(T.ID[:], T.ONB[:], [[-1, 128]], O.is_equal, 0, 1, ["ONB"], ["ID"], 128)
     tk("G", 0.15, [], ["PI"], lambda: g.iota(ICOL["PI"], [[0, 1]], 0, 1))
-    iota(T.IOTAF[:], [[1, VA]], 0, ["IOTAF"], VA)
+    iota(T.IOTAF[:], [[1, VA]], 0, ["IOTAF"], VA, ["BD"])
     iota(T.DUMROW[:], [[1, CAP]], 1024, ["DUMROW"], CAP)
     iota(T.DUMA0[:], [[16, 40]], VA, ["DUMA0"], 40)
+    iota(T.MQ[:], [[0, 8], [1, 16]], 0, ["MQ"], 128)
     asel(T.SLM[:], T.BD[:], [[-1, 128]], O.is_gt, 0, 1, ["BD"], ["SLM"], 128)
     asel(T.SUM[:], T.BD[:], [[1, 128]], O.is_gt, 0, -1, ["BD"], ["SUM"], 128)
     iota(T.JR[:], [[1, CAP]], 0, ["JR"], CAP)
+    for ap, x, n, b in ((T.GS[:, 0:1024], 0, 1024, "GS"), (T.GS[:, 1024:2048], 0, 1024, "GSz"), (T.XA[:, VA:WE], 0, WE - VA, "XAd"), (T.ZROW[:], 0, CAP, "ZROW"),
+                        (T.FL[:], 1, WE, "FL"), (T.C20[:], 20, CAP, "C20"), (T.HB[:], 0, 512, "HB")):
+        iota(ap, [[0, n]], x, [b], n)
+    tk("G", 0.13 + 2 * (WE - VA) * CY, [], ["NBAd"], lambda: g.iota(T.NBA[:, VA:WE], [[0, WE - VA]], 1024, 0))
 
     vms(T.FX[:, S0:VA], 0.0, ["FX"], VA - S0)
     vms(T.FX[:, VA + GH:WE], 0.0, ["FX"], CAP)
@@ -200,24 +206,24 @@ def build(g, core, T, topo, msgs):
     if S_ACT:
         act(T.EF[:], T.EB[:], F.Copy, EBT, ["EF"], 2048)
     vcp(T.EH[:], T.EB[:], EBT, ["EH"], 2048, .5)
-    vms(T.GS[:], 0.0, ["GS"], 2048, .5)
     for q in range(16):
-        vts(T.GS[:, 128 * q + q:128 * q + 128:16], T.BD[:, q:128:16], 32768.0, None, O.mult, None, ["BD", "GS"], ["GS%d" % q], 8)
+        act(T.GS[:, 128 * q + q:128 * q + 128:16], T.BD[:, q:128:16], F.Copy, ["BD", "GS", "GSz"], ["GS%d" % q], 8, scale=32768.0)
         GST.append("GS%d" % q)
-    vts(T.GW[:], T.GS[:], 1.0 / 32768.0, None, O.mult, None, GST, ["GW"], 2048, .5)
     vts(ICOL["PJ"], ICOL["PI"], 15, None, O.bitwise_and, None, ["PI"], ["PJ"], 1)
     vcp(COL["PF"], ICOL["PJ"], ["PJ"], ["PF"], 1)
     vts(T.DUMPA[:], T.DUMA0[:], COL["PF"], None, O.add, None, ["DUMA0", "PF"], ["DUMPA"], 40)
     vts(COL["BIASL"], COL["PF"], -14.5, None, O.add, None, ["PF"], ["BIASL"], 1)
     vts(COL["BIASF"], COL["PF"], -1.0, 0.5, O.mult, O.add, ["PF"], ["BIASF"], 1)
     vts(COL["M0"], COL["PF"], 0.0, -float(ZC), O.is_equal, O.mult, ["PF"], ["M0"], 1)
+    vts(T.BDM[:], T.BD[:], COL["M0"], None, O.mult, None, ["BD", "M0"], ["BDM"], 128)
+    vcp(T.BDH[:], T.BD[:], ["BD"], ["BDH"], 128, .5)
+    vcp(T.SELH[:], T.BD[:, 0:128:16], ["BD"], ["SELH"], 8)
+    vts(T.MASK[:], T.MQ[:], COL["PF"], None, O.is_equal, None, ["MQ", "PF"], ["MASK"], 128)
     vts(COL["M1"], COL["PF"], 1.0, None, O.is_equal, None, ["PF"], ["M1"], 1)
     vts(COL["C0"], COL["PF"], 0.0, 1024.0, O.is_equal, O.mult, ["PF"], ["C0"], 1)
     vts(COL["C2"], COL["PF"], 2.0, -32768.0, O.is_equal, O.mult, ["PF"], ["C2"], 1)
     vtt(COL["C02"], COL["C0"], COL["C2"], O.add, ["C0", "C2"], ["C02"], 1)
     vts(T.DJ[:], T.JR[:], COL["M1"], COL["C02"], O.mult, O.add, ["JR", "M1", "C02"], ["DJ"], CAP)
-    vms(T.ON80[:], 1.0, ["ON80"], 96)
-    vts(T.NEGS[:], T.ON80[:], COL["M0"], None, O.mult, None, ["ON80", "M0"], ["NEGS"], 96)
     vts(T.IDH[:], T.ID[:], 0.5, None, O.mult, None, ["ID"], ["IDH"], 128, .5)
     vtt(T.LU[:], T.IDH[:], T.SLM[:], O.subtract, ["IDH", "SLM"], ["LU"], 128)
     vtt(T.FU[:], T.IDH[:], T.SUM[:], O.subtract, ["IDH", "SUM"], ["FU"], 128)
@@ -225,7 +231,6 @@ def build(g, core, T, topo, msgs):
     vts(T.SLN[:], T.SLM[:], -1.0, None, O.mult, None, ["SLM"], ["SLN"], 128, .5)
     vtt(T.TRIX[:], T.SLN[:], T.IDB[:], O.subtract, ["SLN", "IDB"], ["TRIX"], 128)
     vts(T.BDN[:], T.BD[:], -2048.0, None, O.mult, None, ["BD"], ["BDN"], 128, .5)
-    vms(T.HB[:], 0.0, ["HB"], 512, .5)
     for h in range(2):
         for e in range(2):
             for a in range(4):
@@ -235,12 +240,8 @@ def build(g, core, T, topo, msgs):
     vcp(T.HS[:], T.HB[:], HBT, ["HS"], 512, .5)
     vms(T.O16[:], 1.0 / 16.0, ["O16"], 128)
     vms(T.ONE40[:], 1.0, ["ONE40"], 40)
-    vms(T.C20[:], 20.0, ["C20"], CAP)
-    vms(T.ZROW[:], 0.0, ["ZROW"], CAP)
-    vms(T.FL[:], 1.0, ["FL"], WE)
     vms(T.THR[:, 0:1], 9.0, ["THR0"], 1)
-    vms(T.NBA[:, VA:WE], 1024, ["NBAd"], WE - VA)
-    vms(T.XA[:, VA:WE], 0.0, ["XAd"], WE - VA, .5)
+    vms(T.OBW[:], 0, ["OBW%d%d" % (x, k) for x in range(3) for k in range(3)], 48)
     vms(T.NB[:, 0:OFF], float(NULLC), ["NBf"], OFF)
     vms(T.NB[:, NULLC:WB], float(NULLC), ["NBg"], 8)
     vts(T.TT[:, 240:256], T.ONB[:, 0:16], 1024.0, None, O.mult, None, ["ONB"], ["TTp"], 16)
@@ -265,7 +266,7 @@ def build(g, core, T, topo, msgs):
         arrive("an%d" % i, ["LN%d" % i], 10.0)
     ZBT = ["ZBf", "ZBg", "ZBo", "ZBe0", "ZBe1"]
     NBT = ["NBf", "NBg", "NBo", "NBe0", "NBe1"]
-    B = [T["ps%d" % i] for i in range(8)]
+    B = [T["ps%d" % i] for i in range(7)]
 
     def front(w):
         p = str(w % 2)
@@ -306,7 +307,7 @@ def build(g, core, T, topo, msgs):
         p, s, pa, pb = str(w % 2), str(k), "ps%d" % k, "ps%d" % (3 + k)
         c0, n = CH[k]
         PA, PB = B[k], B[3 + k]
-        cnt, t1, pick, none = PA[:, 0:n], PB[:, 96:96 + n], PB[:, 192:192 + n], PB[:, 288:288 + n]
+        cnt, pick, none = PA[:, 0:n], PB[:, 192:192 + n], PB[:, 288:288 + n]
         tk("V", cost(16 * n, GA), ZBT + ["OFS" + s, "XR" + p + s], ["D" + s],
            lambda: V.tensor_tensor(ch("D", k, 16), T.ZB[:, 0:WB].indirect(ch("OFS", k)), ch("XR" + p, k, 16), O.subtract))
         act(ch("SQ", k, 16), ch("D", k, 16), F.Square, ["D" + s], ["SQ" + s], 16 * n)
@@ -316,23 +317,17 @@ def build(g, core, T, topo, msgs):
         U = "LU" if step else "FU"
         mm([(pick, T[U][:], ch("SG", k), True, True), (none, T.BD[:], ch("SG", k), True, True)], [U, "BD", "SG" + s], [pb], 2 * n)
         act(pick, pick, F.Relu, ["BIASL", "BIASF"], [pb], n, bias=COL["BIASL" if step else "BIASF"])
-        sp = lambda st: T.SP[:, CAP * st + c0:CAP * st + c0 + n]
-        if step == 0:
-            nn, c = ch("NO" + p, k), 4 * (w % 2) + k
-            act(nn, none, F.Relu, [], ["NO" + p + s, pb, "NFAIL%d%d" % (w % 2, k)], n, scale=-0.5, bias=-7.0, accum_out=T.NFAIL[:, c:c + 1])
-            vtt(ch("T2", k), nn, T.NEGS[:, 0:n], O.mult, ["NO" + p + s, "NEGS"], ["T2" + s], n)
-        else:
-            act(none, none, F.Relu, [], [pb], n, scale=-0.5, bias=-7.0)
-            vtt(ch("T2", k), none, sp(step - 1), O.mult, ["SP%s%d" % (s, step - 1)], ["T2" + s, pb], n, 1)
-        vtt(t1, pick, ch("Z", k), O.mult, ["Z" + s], [pb], n, 1)
-        vtt(sp(step), t1, ch("T2", k), O.add, ["T2" + s], ["SP%s%d" % (s, step), pb], n, 1)
-        a, m = CAP * step + c0, n // 16
-        mm([(PB[:, 384:384 + m], T.GW[:, 128 * q:128 * q + 128], T.SP[:, a + q:a + n:16], q == 0, q == 15) for q in range(16)],
-           ["GW", "SP%s%d" % (s, step)], [pb], 1024)
-        if step < 2:
-            vts(T.OBW[:, 8 * k:8 * k + m], PB[:, 384:384 + m], float(ZC), None, O.add, None, [], ["OBW" + s, pb], m)
-        else:
-            vts(T.BW2[:, c0 // 16:c0 // 16 + m], PB[:, 384:384 + m], float(ZC), None, O.add, None, [], ["BW2" + s, pb], m)
+        nn = ch("NO" + p, k) if step == 0 else ch("NN", k)
+        nt = "NO" + p + s if step == 0 else "NN" + s
+        kw = dict(accum_out=T.NFAIL[:, 4 * (w % 2) + k:4 * (w % 2) + k + 1]) if step == 0 else {}
+        act(nn, none, F.Relu, [], [nt, pb] + (["NFAIL%d%d" % (w % 2, k)] if step == 0 else []), n, scale=-0.5, bias=-7.0, **kw)
+        vtt(ch("SP", k), pick, ch("Z", k), O.mult, ["Z" + s], ["SP" + s, pb], n, 1)
+        m, turned, ob = n // 16, PB[0:n, 384:512], PB[:, 96:96 + n // 16]
+        Y = T.Y[0:n, 128 * k:128 * k + 128]
+        mm([(turned, nn, T.BDM[:], True, False), (turned, ch("SP", k), T.BDH[:], False, True)], ["BDM", "BDH", nt, "SP" + s], [pb], 256)
+        vtt(Y, turned, T.MASK[0:n, :], O.mult, ["MASK"], ["Y" + s, pb], 128, 1)
+        mm([(ob, Y, T.SELH[0:n, 0:m], True, True)], ["Y" + s, "SELH"], [pb], 64)
+        vts(T.OBW[:, 16 * step + c0 // 16:16 * step + c0 // 16 + m], ob, float(ZC), None, O.add, None, [], ["OBW%d%s" % (step, s), pb], m)
         cand, ct = (ch("Z", k), "Z") if step == 0 else (ch("OK", k), "OK")
         vtt(cnt, cnt, cand, O.min, [ct + s], [pa], n, 1)
         if step == 0:
@@ -347,18 +342,18 @@ def build(g, core, T, topo, msgs):
         p, s = str(w % 2), str(k)
         c0, n = CH[k]
         nb = (n + 31) // 32
-        mm([(B[7][:, c0:c0 + n], T.BD[:], ch("DJ", k), True, False), (B[7][:, c0:c0 + n], T.BDN[:], ch("SG", k), False, True)],
-           ["BD", "DJ", "BDN", "SG" + s], ["ps7"], 2 * n)
-        vtt(ch("TT", k), ch("NFH" + p, k), B[7][:, c0:c0 + n], O.max, ["NFH" + p], ["TT" + s, "ps7"], n, 1)
+        mm([(B[6][:, c0:c0 + n], T.BD[:], ch("DJ", k), True, False), (B[6][:, c0:c0 + n], T.BDN[:], ch("SG", k), False, True)],
+           ["BD", "DJ", "BDN", "SG" + s], ["ps6"], 2 * n)
+        vtt(ch("TT", k), ch("NFH" + p, k), B[6][:, c0:c0 + n], O.max, ["NFH" + p], ["TT" + s, "ps6"], n, 1)
         tk("V", cost(32 * nb, .5), ["TT" + s, "TTp"], ["TTT" + s], lambda: V.transpose(T.TTT[:, c0:c0 + 32 * nb], T.TT[:, c0:c0 + 32 * nb]))
-        lst = []
-        for q in range(16):
+        lst, z = [], 240 + c0
+        for b in range(nb):
             for h in range(2):
                 for e in range(2):
-                    i, a = 2 * h + e, 240 + c0 + nb * (2 * q + h)
-                    lst.append((B[7][:, a:a + nb], T.HS[:, 128 * i:128 * i + 128], T.TTT[:, c0 + 16 * e + q:c0 + 32 * nb:32], e == 0, e == 1))
-        mm(lst, ["TTT" + s, "HS"], ["ps7"], 4096)
-        vcp(T.FT[:, c0:c0 + 32 * nb], B[7][:, 240 + c0:240 + c0 + 32 * nb], [], ["FT" + s, "ps7"], 32 * nb)
+                    i, a = 2 * h + e, c0 + 32 * b + 16 * e
+                    lst.append((B[6][:, z + h * nb + b:z + 32 * nb:2 * nb], T.HS[:, 128 * i:128 * i + 128], T.TTT[:, a:a + 16], e == 0, e == 1))
+        mm(lst, ["TTT" + s, "HS"], ["ps6"], 64 * len(lst))
+        vcp(T.FT[:, c0:c0 + 32 * nb], B[6][:, z:z + 32 * nb], [], ["FT" + s, "ps6"], 32 * nb)
         for q in range(16):
             a = c0 + 2 * nb * q
             act(T.FL[:, 0:WE].indirect(T.FT[:, a:a + n // 16]), T.C20[:, 0:n], F.Tanh, ["C20", "FT" + s], ["FL"], n, SCA)
@@ -389,19 +384,20 @@ def build(g, core, T, topo, msgs):
             tk("V", cost(CAP, SCA), ["NO%s%d" % (p, k) for k in range(3)] + ["AW" + p], ["EM"],
                lambda: V.tensor_copy(T.EM[:, 0:WE].indirect(AW15), T["NO" + p][:]))
             nf = 4 * (w % 2)
-            mm([(B[7][:, 500:501], T.O16[:], T.NFAIL[:, nf + k:nf + k + 1], k == 0, k == 2) for k in range(3)],
-               ["O16"] + ["NFAIL%d%d" % (w % 2, k) for k in range(3)], ["ps7"], 768)
-            vcp(ICOL["EI"], B[7][:, 500:501], [], ["EI", "ps7"], 1)
+            mm([(B[6][:, 500:501], T.O16[:], T.NFAIL[:, nf + k:nf + k + 1], k == 0, k == 2) for k in range(3)],
+               ["O16"] + ["NFAIL%d%d" % (w % 2, k) for k in range(3)], ["ps6"], 768)
+            vcp(ICOL["EI"], B[6][:, 500:501], [], ["EI", "ps6"], 1)
             vts(ICOL["EJ"], ICOL["EI"], 1, None, O.bitwise_and, None, ["EI"], ["EJ"], 1)
             vts(T.THR[:, w + 1:w + 2], ICOL["EJ"], 7.0, 9.0, O.mult, O.add, ["EJ"], ["THR%d" % (w + 1)], 1)
         for step in (1, 2):
             up = 4096.0 * step
             for k in range(3):
                 s, n = str(k), CH[k][1]
-                tk("V", cost(n, GA), NBT + ["OBW" + s], ["OK" + s],
-                   lambda k=k, n=n, up=up: V.tensor_scalar(ch("OK", k), T.NB[:, 0:WB].indirect(T.OBW[:, 8 * k:8 * k + n // 16]), up, None, op0=O.add))
-                vts(ch("OFS", k), ch("OK", k), -up, None, O.add, None, ["OK" + s], ["OFS" + s], n)
-                act(ch("Z", k), ch("OK", k), F.Copy, ["OK" + s], ["Z" + s], n, bias=-up - ZC)
+                c = 16 * (step - 1) + CH[k][0] // 16
+                nbr, ot = T.NB[:, 0:WB].indirect(T.OBW[:, c:c + n // 16]), "OBW%d%s" % (step - 1, s)
+                vcp(ch("OFS", k), nbr, NBT + [ot], ["OFS" + s], n, GA)
+                act(ch("Z", k), nbr, F.Copy, NBT + [ot], ["Z" + s], n, GA, bias=-float(ZC))
+                act(ch("OK", k), ch("Z", k), F.Copy, ["Z" + s], ["OK" + s], n, bias=up + ZC)
                 test(w, k, step)
         for k in range(3):
             c0, n = CH[k]
@@ -411,12 +407,22 @@ def build(g, core, T, topo, msgs):
             ghosts_out(w + 1)
             front(w + 1)
         XFP = T["XF" + p][:]
-        tk("V", cost(CAP, GA), ZBT + ["BW2%d" % k for k in range(3)] + ["XF" + p], ["XD"],
+        obt = ["OBW%d%d" % (x, k) for x in range(3) for k in range(3)]
+        f = [T.BF[:, 16 * x:16 * x + 15] for x in range(3)]
+        vcp(T.BF[:, 0:47], T.OBW[:, 0:47], obt, ["BF"], 47)
+        vts(T.BM[:, 0:47], T.OBW[:, 0:47], 0.0, None, O.is_equal, None, obt, ["BM"], 47)
+        vtt(T.BS[:, 0:15], f[0], T.BM[:, 16:31], O.mult, ["BF", "BM"], ["BS"], 15)
+        vtt(T.BS[:, 0:15], T.BS[:, 0:15], f[1], O.add, ["BF"], ["BS"], 15)
+        vtt(T.BS[:, 0:15], T.BS[:, 0:15], T.BM[:, 32:47], O.mult, ["BM"], ["BS"], 15)
+        vtt(T.BS[:, 0:15], T.BS[:, 0:15], f[2], O.add, ["BF"], ["BS"], 15)
+        vcp(T.BW2[:, 0:15], T.BS[:, 0:15], ["BS"], ["BW2"], 15)
+        tk("V", cost(CAP, GA), ZBT + ["BW2", "XF" + p], ["XD"],
            lambda: V.tensor_tensor(T.XD[:], T.ZB[:, 0:WB].indirect(T.BW2[:, 0:15]), XFP, O.subtract))
         vts(T.XC[:], T.XD[:], -2.0, 2.0, O.max, O.min, ["XD"], ["XC"], CAP, .5)
-        act(T.SC[:], T["NO" + p][:], F.Copy, ["NO%s%d" % (p, k) for k in range(3)], ["SC"], CAP, scale=-1.0, bias=1.0)
-        vtt(T.XM[:], T.XC[:], T.SC[:], O.mult, ["XC", "SC"], ["XM"], CAP)
-        vtt(T.XN[:], T.XM[:], XFP, O.add, ["XM", "XF" + p], ["XN"], CAP)
+        SC = B[5][:, 0:CAP]
+        act(SC, T["NO" + p][:], F.Copy, ["NO%s%d" % (p, k) for k in range(3)], ["ps5"], CAP, scale=-1.0, bias=1.0)
+        vtt(SC, SC, T.XC[:], O.mult, ["XC"], ["ps5"], CAP, 1)
+        vtt(T.XN[:], SC, XFP, O.add, ["XF" + p], ["XN", "ps5"], CAP, 1)
         tk("V", cost(CAP, SCA), ["XN", "AW" + p], ["XA"], lambda: V.tensor_copy(T.XA[:, 0:WE].indirect(AW15), T.XN[:]))
 
     for w in range(RO):
@@ -430,6 +436,8 @@ def build(g, core, T, topo, msgs):
 
 
 LAT = {"V": 0.05, "A": 0.08, "P": 0.1, "G": 0.1, None: 0.0}
+EPS = 0.06
+BONUS = {}
 
 
 def plan(tasks):
@@ -442,6 +450,7 @@ def plan(tasks):
     prio = [0.0] * n
     for i in range(n - 1, -1, -1):
         prio[i] = tasks[i]["dur"] + lat[i] + max([prio[j] for j in succ[i]] + [0.0])
+    prio = [p + BONUS.get(t["tag"], 0.0) for p, t in zip(prio, tasks)]
     left = [len(t["deps"]) for t in tasks]
     est, fin, free, order = [0.0] * n, [0.0] * n, {}, []
     ready = {}
@@ -455,7 +464,7 @@ def plan(tasks):
                 continue
             f = free.get(q, 0.0) if q is not None else 0.0
             t0 = min(max(f, est[i]) for i in lst)
-            c = max((i for i in lst if max(f, est[i]) <= t0 + 0.06), key=lambda i: prio[i])
+            c = max((i for i in lst if max(f, est[i]) <= t0 + EPS), key=lambda i: prio[i])
             if best is None or t0 < best[0]:
                 best = (t0, q, c)
         t0, q, i = best

from concourse.mybir import AluOpType as O, ActivationFunctionType as F

VA, GH, OB, CAP, S0, RO = 640, 384, 1280, 240, 176, 5
OFF, NULLC, ZC = 9, 2568, 1288
EXT = OFF + OB
WB = 2576
WE = 1264
NB_HALF = 640
CH = ((0, 96), (96, 64), (160, 80))
S_ACT = (1,)

SCRATCH = {}
_L = {
    "bfloat16": "ZB:2576 XA:1264 EM:1264 FLB:640 MB:176 ONB:128 BD:128 BDT:128 ID:128 SLM:128 SUM:128 LU:128 FU:128 IDH:128 IDB:128 "
                "SLN:128 TRIX:128 BDN:128 BDM:128 GS:2048 EB:2048 HB:512 DJ:240 EL:40 XD:240 XC:240 XN:240 RX:640 "
                "XR0:3840 XR1:3840 XF0:240 XF1:240 NO0:240 NO1:240 D:3840 SQ:3840 NR:3840 SG:240 NN:240",
    "float16": "LWH:240 BDH:128 SELH:8 Y:384 EH:2048 HS:512 TT:256 TTT:256 NFH0:240 NFH1:240 ST:3840 SP:240",
    "float32": "NB:2576 FX:1264 FL:1264 LW:1280 MF:176 FA:176 EF:2048 O16:128 COL:8 JR:240 MQ:128 MASK:128 BF:48 BM:48 BS:16 "
               "DUMROW:240 IOTAF:640 DUMA0:40 DUMPA:40 C20:240 ZROW:240 ONE40:40 CUM:40 PO1:40 PO2:40 THR:8 NFAIL:16 "
               "YM:640 Y1:640 YO:640 SF:3840 Z:240 OK:240 NW:240 NX:240",
    "int32": "NBB:1280 NBA:1264 F0I:176 BDI:24 ICOL:4 KI:240 NI:240",
    "uint16": "NBX:1280 LN:1280 BDU:24 POU:40 FT:256 BW2:16 RN:640 GHS:1920 RG:1920 LG:1920 NFU0:240 NFU1:240 AW0:16 AW1:16 "
              "LU0:240 LU1:240 OFS:240 OBW:48",
}
for _d in _L:
    for _x in _L[_d].split():
        SCRATCH[_x.split(":")[0]] = ("sbuf", [128, int(_x.split(":")[1])], _d)
for _i in range(7):
    SCRATCH["ps%d" % _i] = ("psum", [128, 512], "float32")

LOADS = ["xb", "f0", "bd", "nba", "xa", "nbb"]
SEMAPHORES = ["sV", "sA", "sP", "sG", "ls", "oy", "ox", "rx", "rn", "ax0", "ax1", "an0", "an1"] + \
    ["l" + n for n in LOADS] + ["rg%d" % w for w in range(RO)] + ["ag%d" % w for w in range(RO)]


def relays(topo, src, dst):
    c = [x for x in topo.cores_of(src) if x != src and topo.may_write(x, dst)]
    return sorted(c, key=lambda x: (topo.die(x) != topo.die(src), x))


def messages(topo, cores):
    n, out = len(cores), []
    for r in range(n):
        src, prev, nxt = cores[r], cores[(r - 1) % n], cores[(r + 1) % n]
        rb = relays(topo, src, prev)
        w = (NB_HALF, OB - 1 - NB_HALF)
        for i in range(2):
            a, b = i * NB_HALF, i * NB_HALF + w[i]
            out.append((src, rb[i], prev, "RX", (0, w[i]), "rx", "ZB", (EXT + a, EXT + b), "ax%d" % i, "ZB", (OFF + a, OFF + b)))
        for i in range(2):
            a, b = i * NB_HALF, i * NB_HALF + w[i]
            out.append((src, rb[2 + i], prev, "RN", (0, w[i]), "rn", "LN", (a, b), "an%d" % i, "NBX", (a, b)))
        rg = relays(topo, src, nxt)
        for k in range(RO):
            s = (k * GH, (k + 1) * GH)
            out.append((src, rg[0], nxt, "RG", s, "rg%d" % k, "LG", s, "ag%d" % k, "GHS", s))
    return out


def send(g, topo, src, dst, dbuf, dcol, sbuf, scol, T, rsem):
    rid, pid = topo.addr(dst, src)
    g.remote_dma(T[dbuf][:, dcol[0]:dcol[1]], T[sbuf][:, scol[0]:scol[1]], T.sem[rsem], T.sem["ls"], pid, rid, topo.mask(src, dst))
    return len(topo.engines(src, dst))


def relay_program(g, core, T, topo, msgs):
    total = 0
    for m in msgs:
        if m[1] == core:
            g.wait_ge(T.sem[m[5]], len(topo.engines(m[0], core)))
            total += send(g, topo, core, m[2], m[6], m[7], m[3], m[4], T, m[8])
    if total:
        g.wait_ge(T.sem["ls"], total)


CY = 0.00083 * 1.25
GA, SCA = 1.5, 3.6


def build(g, core, T, topo, msgs):
    tasks, lastw, readers = [], {}, {}
    V, A, P, SY = g.vector, g.scalar, g.tensor, g.sync
    COL = {x: T.COL[:, i:i + 1] for i, x in enumerate(("PF", "BIASL", "BIASF", "M0", "M1", "C0", "C2", "C02"))}
    ICOL = {x: T.ICOL[:, i:i + 1] for i, x in enumerate(("PI", "PJ", "EI", "EJ"))}

    def tk(q, dur, rd, wr, fn, sem=None, val=0):
        deps = {}
        i = len(tasks)
        for b in rd:
            if b in lastw:
                deps[lastw[b]] = True
        for b in wr:
            if b in lastw:
                deps[lastw[b]] = True
            for x in readers.get(b, []):
                deps.setdefault(x, False)
        for b in rd:
            if b not in wr:
                readers.setdefault(b, []).append(i)
        for b in wr:
            lastw[b] = i
            readers[b] = []
        tag = "".join(x for x in wr[0] if x.isalpha()) + (q or "")
        tasks.append(dict(q=q, dur=dur, deps=deps, fn=fn, sem=sem, val=val, tag=tag))

    def cost(n, c):
        return 0.06 + max(64, n * c) * CY

    def vts(out, in0, s1, s2, o0, o1, rd, wr, n, c=1.0):
        if o1 is None:
            tk("V", cost(n, c), rd, wr, lambda: V.tensor_scalar(out, in0, s1, None, op0=o0))
        else:
            tk("V", cost(n, c), rd, wr, lambda: V.tensor_scalar(out, in0, s1, s2, op0=o0, op1=o1))

    def vtt(out, a, b, op, rd, wr, n, c=2.0):
        tk("V", cost(n, c), rd, wr, lambda: V.tensor_tensor(out, a, b, op))

    def vcp(out, in_, rd, wr, n, c=1.0):
        tk("V", cost(n, c), rd, wr, lambda: V.tensor_copy(out, in_))

    def vms(ap, x, wr, n, c=1.0):
        tk("V", cost(n, c), [], wr, lambda: V.memset(ap, x))

    def act(out, in_, fn, rd, wr, n, c=1.0, **kw):
        tk("A", 0.07 + n * c * CY, rd, wr, lambda: A.activation(out, in_, fn, **kw))

    def mm(lst, rd, wr, cyc):
        def fn():
            x = None
            for o, l, r, a, b in lst:
                x = P.matmul(o, l, r, a, b)
            return x
        tk("P", 0.05 + cyc * 0.00075, rd, wr, fn)

    def iota(out, pat, base, wr, n, rd=()):
        tk("G", 0.13 + 2 * n * CY, list(rd), wr, lambda: g.iota(out, pat, base, 0, allow_small_or_imprecise_dtypes=True))

    def asel(out, in_, pat, op, base, cm, rd, wr, n):
        tk("G", 0.17 + 2 * n * CY, rd, wr, lambda: g.affine_select(out, in_, pat, op, 0.0, base, cm))

    def ch(name, k, w=1):
        return T[name][:, w * CH[k][0]:w * (CH[k][0] + CH[k][1])]

    def by(name, k, q):
        return T[name][:, 16 * CH[k][0] + q:16 * (CH[k][0] + CH[k][1]):16]

    def load(q, name, out, wr, rd):
        e = SY if q == "S" else A
        tk(q, 0.1, rd, wr, lambda: e.dma_start(out, T[name][:]), sem="l" + name, val=16)

    vms(T.ZB[:, 0:OFF], 1000.0, ["ZBf"], OFF)
    vms(T.ZB[:, NULLC:WB], 1000.0, ["ZBg"], 8)
    load("S", "f0", T.F0I[:], ["F0I"], [])
    load("A", "xb", T.ZB[:, OFF:EXT], ["ZBo"], ["ZBf"])
    load("S", "bd", T.BDI[:], ["BDI"], [])
    load("S", "nba", T.NBA[:, 0:VA], ["NBA"], [])
    load("A", "xa", T.XA[:, 0:VA], ["XA"], [])
    load("S", "nbb", T.NBB[:], ["NBB"], [])

    mine = [m for m in msgs if m[0] == core]
    inb = {m[8]: m for m in msgs if m[2] == core}
    sent = [0]

    def remote(m, rd):
        def fn():
            sent[0] += send(g, topo, core, m[1], m[3], m[4], m[9], m[10], T, m[5])
        tk("G", 0.6, rd, ["snt" + m[8]], fn, sem="none")

    def arrive(sem, wr, delay):
        m = inb[sem]
        tk(None, delay, ["snt" + sem], wr, None, sem=sem, val=len(topo.engines(m[1], core)))

    for m in mine[0:2]:
        remote(m, ["ZBo"])

    vms(T.ONB[:], 1.0, ["ONB"], 128, .5)
    asel(T.BDT[:], T.ONB[:], [[-16, 8], [0, 16]], O.is_ge, 0, 1, ["ONB"], ["BDT"], 128)
    asel(T.BD[:], T.BDT[:], [[16, 8], [0, 16]], O.is_ge, 15, -1, ["BDT"], ["BD"], 128)
    asel(T.ID[:], T.ONB[:], [[-1, 128]], O.is_equal, 0, 1, ["ONB"], ["ID"], 128)
    tk("G", 0.15, [], ["PI"], lambda: g.iota(ICOL["PI"], [[0, 1]], 0, 1))
    iota(T.IOTAF[:], [[1, VA]], 0, ["IOTAF"], VA, ["BD"])
    iota(T.DUMROW[:], [[1, CAP]], 1024, ["DUMROW"], CAP)
    iota(T.DUMA0[:], [[16, 40]], VA, ["DUMA0"], 40)
    iota(T.MQ[:], [[0, 8], [1, 16]], 0, ["MQ"], 128)
    asel(T.SLM[:], T.BD[:], [[-1, 128]], O.is_gt, 0, 1, ["BD"], ["SLM"], 128)
    asel(T.SUM[:], T.BD[:], [[1, 128]], O.is_gt, 0, -1, ["BD"], ["SUM"], 128)
    iota(T.JR[:], [[1, CAP]], 0, ["JR"], CAP)
    for ap, x, n, b in ((T.GS[:, 0:1024], 0, 1024, "GS"), (T.GS[:, 1024:2048], 0, 1024, "GSz"), (T.XA[:, VA:WE], 0, WE - VA, "XAd"), (T.ZROW[:], 0, CAP, "ZROW"),
                        (T.FL[:], 1, WE, "FL"), (T.C20[:], 20, CAP, "C20"), (T.HB[:], 0, 512, "HB")):
        iota(ap, [[0, n]], x, [b], n)
    tk("G", 0.13 + 2 * (WE - VA) * CY, [], ["NBAd"], lambda: g.iota(T.NBA[:, VA:WE], [[0, WE - VA]], 1024, 0))

    vms(T.FX[:, S0:VA], 0.0, ["FX"], VA - S0)
    vms(T.FX[:, VA + GH:WE], 0.0, ["FX"], CAP)
    vts(T.MF[:], T.F0I[:], 2559, None, O.is_lt, None, ["F0I"], ["MF"], S0)
    vts(T.FA[:], T.F0I[:], OFF, None, O.add, None, ["F0I"], ["FA"], S0)
    vtt(T.FX[:, 0:S0], T.FA[:], T.MF[:], O.mult, ["FA", "MF"], ["FX"], S0)
    vcp(T.BDU[:], T.BDI[:], ["BDI"], ["BDU"], 24)
    vcp(T.MB[:], T.MF[:], ["MF"], ["MB"], S0)
    vms(T.EM[:], 1.0, ["EM"], WE, .5)
    vms(T.EB[:], 0.0, ["EB"], 2048, .5)
    EBT, GST, HBT = ["EB"], ["GS"], ["HB"]
    for q in range(16):
        act(T.EB[:, 128 * q + q:128 * q + 128:16], T.ID[:, q:128:16], F.Copy, ["ID", "EB"], ["EB%d" % q], 8)
        EBT.append("EB%d" % q)
    if S_ACT:
        act(T.EF[:], T.EB[:], F.Copy, EBT, ["EF"], 2048)
    vcp(T.EH[:], T.EB[:], EBT, ["EH"], 2048, .5)
    for q in range(16):
        act(T.GS[:, 128 * q + q:128 * q + 128:16], T.BD[:, q:128:16], F.Copy, ["BD", "GS", "GSz"], ["GS%d" % q], 8, scale=32768.0)
        GST.append("GS%d" % q)
    vts(ICOL["PJ"], ICOL["PI"], 15, None, O.bitwise_and, None, ["PI"], ["PJ"], 1)
    vcp(COL["PF"], ICOL["PJ"], ["PJ"], ["PF"], 1)
    vts(T.DUMPA[:], T.DUMA0[:], COL["PF"], None, O.add, None, ["DUMA0", "PF"], ["DUMPA"], 40)
    vts(COL["BIASL"], COL["PF"], -14.5, None, O.add, None, ["PF"], ["BIASL"], 1)
    vts(COL["BIASF"], COL["PF"], -1.0, 0.5, O.mult, O.add, ["PF"], ["BIASF"], 1)
    vts(COL["M0"], COL["PF"], 0.0, -float(ZC), O.is_equal, O.mult, ["PF"], ["M0"], 1)
    vts(T.BDM[:], T.BD[:], COL["M0"], None, O.mult, None, ["BD", "M0"], ["BDM"], 128)
    vcp(T.BDH[:], T.BD[:], ["BD"], ["BDH"], 128, .5)
    vcp(T.SELH[:], T.BD[:, 0:128:16], ["BD"], ["SELH"], 8)
    vts(T.MASK[:], T.MQ[:], COL["PF"], None, O.is_equal, None, ["MQ", "PF"], ["MASK"], 128)
    vts(COL["M1"], COL["PF"], 1.0, None, O.is_equal, None, ["PF"], ["M1"], 1)
    vts(COL["C0"], COL["PF"], 0.0, 1024.0, O.is_equal, O.mult, ["PF"], ["C0"], 1)
    vts(COL["C2"], COL["PF"], 2.0, -32768.0, O.is_equal, O.mult, ["PF"], ["C2"], 1)
    vtt(COL["C02"], COL["C0"], COL["C2"], O.add, ["C0", "C2"], ["C02"], 1)
    vts(T.DJ[:], T.JR[:], COL["M1"], COL["C02"], O.mult, O.add, ["JR", "M1", "C02"], ["DJ"], CAP)
    vts(T.IDH[:], T.ID[:], 0.5, None, O.mult, None, ["ID"], ["IDH"], 128, .5)
    vtt(T.LU[:], T.IDH[:], T.SLM[:], O.subtract, ["IDH", "SLM"], ["LU"], 128)
    vtt(T.FU[:], T.IDH[:], T.SUM[:], O.subtract, ["IDH", "SUM"], ["FU"], 128)
    vts(T.IDB[:], T.ID[:], 2048.0, None, O.mult, None, ["ID"], ["IDB"], 128, .5)
    vts(T.SLN[:], T.SLM[:], -1.0, None, O.mult, None, ["SLM"], ["SLN"], 128, .5)
    vtt(T.TRIX[:], T.SLN[:], T.IDB[:], O.subtract, ["SLN", "IDB"], ["TRIX"], 128)
    vts(T.BDN[:], T.BD[:], -2048.0, None, O.mult, None, ["BD"], ["BDN"], 128, .5)
    for h in range(2):
        for e in range(2):
            for a in range(4):
                c = 128 * (2 * h + e) + 32 * a + 16 * e
                HBT.append("HB%d" % c)
                act(T.HB[:, c:c + 16], T.ID[:, 32 * a + 16 * h:32 * a + 16 * h + 16], F.Copy, ["ID", "HB"], [HBT[-1]], 16)
    vcp(T.HS[:], T.HB[:], HBT, ["HS"], 512, .5)
    vms(T.O16[:], 1.0 / 16.0, ["O16"], 128)
    vms(T.ONE40[:], 1.0, ["ONE40"], 40)
    vms(T.THR[:, 0:1], 9.0, ["THR0"], 1)
    vms(T.OBW[:], 0, ["OBW%d%d" % (x, k) for x in range(3) for k in range(3)], 48)
    vms(T.NB[:, 0:OFF], float(NULLC), ["NBf"], OFF)
    vms(T.NB[:, NULLC:WB], float(NULLC), ["NBg"], 8)
    vts(T.TT[:, 240:256], T.ONB[:, 0:16], 1024.0, None, O.mult, None, ["ONB"], ["TTp"], 16)

    def ghosts_out(w):
        vts(T.GHS[:, w * GH:(w + 1) * GH], T.FX[:, 0:VA].indirect(T.BDU[:, 0:24]), float(OB + 8), -float(OB), O.max, O.add,
            ["FX", "BDU"], ["GHS%d" % w], GH, GA)
        remote(mine[4 + w], ["GHS%d" % w])

    def ghosts_in(w):
        arrive("ag%d" % w, ["LG%d" % w], 4.0)
        vcp(T.FX[:, VA:VA + GH], T.LG[:, w * GH:(w + 1) * GH], ["LG%d" % w], ["FX"], GH)

    ghosts_out(0)
    vts(T.NBX[:], T.NBB[:], EXT, NULLC, O.add, O.min, ["NBB"], ["NBX"], OB)
    for m in mine[2:4]:
        remote(m, ["NBX"])
    vts(T.NB[:, OFF:EXT], T.NBB[:], OFF, None, O.add, None, ["NBB"], ["NBo"], OB)
    for i in range(2):
        arrive("ax%d" % i, ["ZBe%d" % i], 8.0)
    for i in range(2):
        arrive("an%d" % i, ["LN%d" % i], 10.0)
    ZBT = ["ZBf", "ZBg", "ZBo", "ZBe0", "ZBe1"]
    NBT = ["NBf", "NBg", "NBo", "NBe0", "NBe1"]
    B = [T["ps%d" % i] for i in range(7)]

    def front(w):
        p = str(w % 2)
        el = B[6][:, 0:40]
        if w == 0:
            mm([(B[6][:, 40:40 + S0], T.BD[:], T.MB[:], True, True)], ["BD", "MB"], ["ps6"], S0)
            vts(T.EM[:, 0:S0], B[6][:, 40:40 + S0], 0.0, None, O.is_equal, None, ["ps6"], ["EM", "ps6"], S0)
        mm([(el, T.EB[:, 128 * q:128 * q + 128], T.EM[:, q:VA:16], q == 0, w == 0 and q == 15) for q in range(16)], ["EM"] + EBT, ["ps6"], 1024)
        if w:
            act(T.FLB[:], T.FL[:, 0:VA], F.Copy, ["FL"], ["FLB"], VA)
            mm([(el, T.EB[:, 128 * q:128 * q + 128], T.FLB[:, q:VA:16], False, q == 15) for q in range(16)], ["FLB"] + EBT, ["ps6"], 1024)
        vts(T.EL[:], el, 1.5 if w else 0.5, None, O.is_ge, None, ["ps6"], ["EL", "ps6"], 40)
        mm([(B[6][:, 40:80], T.BD[:], T.EL[:], True, True), (B[6][:, 80:120], T.TRIX[:], T.EL[:], True, True)], ["BD", "TRIX", "EL"], ["ps6"], 128)
        tk("V", cost(40, 1), ["ONE40"], ["CUM", "ps6"], lambda: V.tensor_tensor_scan(T.CUM[:], T.ONE40[:], B[6][:, 40:80], 2047.0, O.mult, O.add))
        vtt(T.PO1[:], T.CUM[:], B[6][:, 80:120], O.add, ["CUM"], ["PO1", "ps6"], 40, 1)
        vtt(T.PO2[:], T.PO1[:], T.DUMPA[:], O.min, ["PO1", "DUMPA"], ["PO2"], 40)
        vcp(T.POU[:], T.PO2[:], ["PO2"], ["POU"], 40)
        act(T.LW[:, 0:CAP], T.DUMROW[:], F.Copy, ["DUMROW"], ["LW"], CAP)
        tk("V", cost(VA, SCA), ["POU", "IOTAF"], ["LW"], lambda: V.tensor_copy(T.LW[:, 0:1280].indirect(T.POU[:, 0:40]), T.IOTAF[:]))
        vcp(T.LWH[:], T.LW[:, 0:CAP], ["LW"], ["LWH"], CAP)
        mm([(B[6][:, 120:135], T.EH[:, 128 * q:128 * q + 128], T.LWH[:, q:CAP:16], q == 0, q == 15) for q in range(16)], ["LWH", "EH"], ["ps6"], 1024)
        vcp(T["LU" + p][:], T.LW[:, 0:CAP], ["LW"], ["LU" + p], CAP)
        vcp(T["AW" + p][:, 0:15], B[6][:, 120:135], [], ["AW" + p, "ps6"], 15)
        vcp(T["NFU" + p][:], T.NBA[:, 0:WE].indirect(T["AW" + p][:, 0:15]), ["NBA", "NBAd", "AW" + p], ["NFU" + p], CAP, GA)
        vcp(T["NFH" + p][:], T["NFU" + p][:], ["NFU" + p], ["NFH" + p], CAP, .5)
        act(T["XF" + p][:], T.XA[:, 0:WE].indirect(T["AW" + p][:, 0:15]), F.Copy, ["XA", "XAd", "AW" + p], ["XF" + p], CAP, GA)
        for k in range(3):
            act(ch("XR" + p, k, 16), T.XA[:, 0:WE].indirect(ch("LU" + p, k)), F.Copy, ["XA", "XAd", "LU" + p], ["XR%s%d" % (p, k)], 16 * CH[k][1], GA)
        if w < RO - 1:
            act(T.FL[:, 0:WE].indirect(T["AW" + p][:, 0:15]), T.ZROW[:], F.Tanh, ["ZROW", "AW" + p], ["FL"], CAP, SCA)

    front(0)
    for i in range(2):
        a, b = (0, NB_HALF) if i == 0 else (NB_HALF, OB - 1)
        vcp(T.NB[:, EXT + a:EXT + b], T.LN[:, a:b], ["LN%d" % i], ["NBe%d" % i], b - a)

    def test(w, k, step):
        p, s, pa, pb = str(w % 2), str(k), "ps%d" % k, "ps%d" % (3 + k)
        c0, n = CH[k]
        PA, PB = B[k], B[3 + k]
        cnt, pick, none = PA[:, 0:n], PB[:, 192:192 + n], PB[:, 288:288 + n]
        tk("V", cost(16 * n, GA), ZBT + ["OFS" + s, "XR" + p + s], ["D" + s],
           lambda: V.tensor_tensor(ch("D", k, 16), T.ZB[:, 0:WB].indirect(ch("OFS", k)), ch("XR" + p, k, 16), O.subtract))
        act(ch("SQ", k, 16), ch("D", k, 16), F.Square, ["D" + s], ["SQ" + s], 16 * n)
        vts(ch("NR", k, 16), ch("SQ", k, 16), T.THR[:, w:w + 1], 0.84375, O.is_le, O.subtract, ["SQ" + s, "THR%d" % w], ["NR" + s], 16 * n, .5)
        mm([(cnt, T.GS[:, 128 * q:128 * q + 128], by("NR", k, q), q == 0, q == 15) for q in range(16)], ["NR" + s] + GST, [pa], 16 * n)
        act(ch("SG", k), cnt, F.Sign, [], ["SG" + s, pa], n)
        U = "LU" if step else "FU"
        mm([(pick, T[U][:], ch("SG", k), True, True), (none, T.BD[:], ch("SG", k), True, True)], [U, "BD", "SG" + s], [pb], 2 * n)
        act(pick, pick, F.Relu, ["BIASL", "BIASF"], [pb], n, bias=COL["BIASL" if step else "BIASF"])
        nn = ch("NO" + p, k) if step == 0 else ch("NN", k)
        nt = "NO" + p + s if step == 0 else "NN" + s
        kw = dict(accum_out=T.NFAIL[:, 4 * (w % 2) + k:4 * (w % 2) + k + 1]) if step == 0 else {}
        act(nn, none, F.Relu, [], [nt, pb] + (["NFAIL%d%d" % (w % 2, k)] if step == 0 else []), n, scale=-0.5, bias=-7.0, **kw)
        vtt(ch("SP", k), pick, ch("Z", k), O.mult, ["Z" + s], ["SP" + s, pb], n, 1)
        m, turned, ob = n // 16, PB[0:n, 384:512], PB[:, 96:96 + n // 16]
        Y = T.Y[0:n, 128 * k:128 * k + 128]
        mm([(turned, nn, T.BDM[:], True, False), (turned, ch("SP", k), T.BDH[:], False, True)], ["BDM", "BDH", nt, "SP" + s], [pb], 256)
        vtt(Y, turned, T.MASK[0:n, :], O.mult, ["MASK"], ["Y" + s, pb], 128, 1)
        mm([(ob, Y, T.SELH[0:n, 0:m], True, True)], ["Y" + s, "SELH"], [pb], 64)
        vts(T.OBW[:, 16 * step + c0 // 16:16 * step + c0 // 16 + m], ob, float(ZC), None, O.add, None, [], ["OBW%d%s" % (step, s), pb], m)
        cand, ct = (ch("Z", k), "Z") if step == 0 else (ch("OK", k), "OK")
        vtt(cnt, cnt, cand, O.min, [ct + s], [pa], n, 1)
        if step == 0:
            vts(ch("NW", k), cnt, -float(ZC), float(ZC), O.max, O.add, [], ["NW" + s, pa], n)
        elif step == 1:
            vtt(ch("NX", k), ch("NW", k), cnt, O.max, ["NW" + s], ["NX" + s, pa], n, 1)
        else:
            vtt(ch("KI", k), ch("NX", k), cnt, O.max, ["NX" + s], ["KI" + s, pa], n, 1)
            vts(ch("NI", k), ch("KI", k), 4095, None, O.bitwise_and, None, ["KI" + s], ["NI" + s], n)

    def mark(w, k):
        p, s = str(w % 2), str(k)
        c0, n = CH[k]
        nb = (n + 31) // 32
        mm([(B[6][:, c0:c0 + n], T.BD[:], ch("DJ", k), True, False), (B[6][:, c0:c0 + n], T.BDN[:], ch("SG", k), False, True)],
           ["BD", "DJ", "BDN", "SG" + s], ["ps6"], 2 * n)
        vtt(ch("TT", k), ch("NFH" + p, k), B[6][:, c0:c0 + n], O.max, ["NFH" + p], ["TT" + s, "ps6"], n, 1)
        tk("V", cost(32 * nb, .5), ["TT" + s, "TTp"], ["TTT" + s], lambda: V.transpose(T.TTT[:, c0:c0 + 32 * nb], T.TT[:, c0:c0 + 32 * nb]))
        lst, z = [], 240 + c0
        for b in range(nb):
            for h in range(2):
                for e in range(2):
                    i, a = 2 * h + e, c0 + 32 * b + 16 * e
                    lst.append((B[6][:, z + h * nb + b:z + 32 * nb:2 * nb], T.HS[:, 128 * i:128 * i + 128], T.TTT[:, a:a + 16], e == 0, e == 1))
        mm(lst, ["TTT" + s, "HS"], ["ps6"], 64 * len(lst))
        vcp(T.FT[:, c0:c0 + 32 * nb], B[6][:, z:z + 32 * nb], [], ["FT" + s, "ps6"], 32 * nb)
        for q in range(16):
            a = c0 + 2 * nb * q
            act(T.FL[:, 0:WE].indirect(T.FT[:, a:a + n // 16]), T.C20[:, 0:n], F.Tanh, ["C20", "FT" + s], ["FL"], n, SCA)

    def wave(w):
        p = str(w % 2)
        last = w == RO - 1
        AW15 = T["AW" + p][:, 0:15]
        ghosts_in(w)
        for k in range(3):
            s = str(k)
            c0, n = CH[k]
            PA = B[k]
            off = ch("NFU" + p, k)
            if k in S_ACT:
                act(ch("SF", k, 16), T.FX[:, 0:WE].indirect(off), F.Copy, ["FX", "NFU" + p], ["SF" + s], 16 * n, GA, bias=-float(ZC))
                src, E, cyc = "SF", "EF", 64 * n
            else:
                vts(ch("ST", k, 16), T.FX[:, 0:WE].indirect(off), -float(ZC), None, O.add, None, ["FX", "NFU" + p], ["ST" + s], 16 * n, GA)
                src, E, cyc = "ST", "EH", 16 * n
            mm([(PA[:, 96:96 + n], T[E][:, 128 * q:128 * q + 128], by(src, k, q), q == 0, q == 15) for q in range(16)], [src + s, E], ["ps%d" % k], cyc)
            vts(ch("OFS", k), PA[:, 96:96 + n], float(ZC), None, O.add, None, [], ["OFS" + s, "ps%d" % k], n)
            act(ch("Z", k), PA[:, 96:96 + n], F.Copy, [], ["Z" + s, "ps%d" % k], n)
            test(w, k, 0)
            if not last:
                mark(w, k)
        if not last:
            tk("V", cost(CAP, SCA), ["NO%s%d" % (p, k) for k in range(3)] + ["AW" + p], ["EM"],
               lambda: V.tensor_copy(T.EM[:, 0:WE].indirect(AW15), T["NO" + p][:]))
            nf = 4 * (w % 2)
            mm([(B[6][:, 500:501], T.O16[:], T.NFAIL[:, nf + k:nf + k + 1], k == 0, k == 2) for k in range(3)],
               ["O16"] + ["NFAIL%d%d" % (w % 2, k) for k in range(3)], ["ps6"], 768)
            vcp(ICOL["EI"], B[6][:, 500:501], [], ["EI", "ps6"], 1)
            vts(ICOL["EJ"], ICOL["EI"], 1, None, O.bitwise_and, None, ["EI"], ["EJ"], 1)
            vts(T.THR[:, w + 1:w + 2], ICOL["EJ"], 7.0, 9.0, O.mult, O.add, ["EJ"], ["THR%d" % (w + 1)], 1)
        for step in (1, 2):
            up = 4096.0 * step
            for k in range(3):
                s, n = str(k), CH[k][1]
                c = 16 * (step - 1) + CH[k][0] // 16
                nbr, ot = T.NB[:, 0:WB].indirect(T.OBW[:, c:c + n // 16]), "OBW%d%s" % (step - 1, s)
                vcp(ch("OFS", k), nbr, NBT + [ot], ["OFS" + s], n, GA)
                act(ch("Z", k), nbr, F.Copy, NBT + [ot], ["Z" + s], n, GA, bias=-float(ZC))
                act(ch("OK", k), ch("Z", k), F.Copy, ["Z" + s], ["OK" + s], n, bias=up + ZC)
                test(w, k, step)
        for k in range(3):
            c0, n = CH[k]
            tk("V", cost(n, SCA), ["NI%d" % k, "AW" + p], ["FX"],
               lambda k=k, c0=c0, n=n: V.tensor_copy(T.FX[:, 0:WE].indirect(T["AW" + p][:, c0 // 16:(c0 + n) // 16]), ch("NI", k)))
        if not last:
            ghosts_out(w + 1)
            front(w + 1)
        XFP = T["XF" + p][:]
        obt = ["OBW%d%d" % (x, k) for x in range(3) for k in range(3)]
        f = [T.BF[:, 16 * x:16 * x + 15] for x in range(3)]
        vcp(T.BF[:, 0:47], T.OBW[:, 0:47], obt, ["BF"], 47)
        vts(T.BM[:, 0:47], T.OBW[:, 0:47], 0.0, None, O.is_equal, None, obt, ["BM"], 47)
        vtt(T.BS[:, 0:15], f[0], T.BM[:, 16:31], O.mult, ["BF", "BM"], ["BS"], 15)
        vtt(T.BS[:, 0:15], T.BS[:, 0:15], f[1], O.add, ["BF"], ["BS"], 15)
        vtt(T.BS[:, 0:15], T.BS[:, 0:15], T.BM[:, 32:47], O.mult, ["BM"], ["BS"], 15)
        vtt(T.BS[:, 0:15], T.BS[:, 0:15], f[2], O.add, ["BF"], ["BS"], 15)
        vcp(T.BW2[:, 0:15], T.BS[:, 0:15], ["BS"], ["BW2"], 15)
        tk("V", cost(CAP, GA), ZBT + ["BW2", "XF" + p], ["XD"],
           lambda: V.tensor_tensor(T.XD[:], T.ZB[:, 0:WB].indirect(T.BW2[:, 0:15]), XFP, O.subtract))
        vts(T.XC[:], T.XD[:], -2.0, 2.0, O.max, O.min, ["XD"], ["XC"], CAP, .5)
        SC = B[5][:, 0:CAP]
        act(SC, T["NO" + p][:], F.Copy, ["NO%s%d" % (p, k) for k in range(3)], ["ps5"], CAP, scale=-1.0, bias=1.0)
        vtt(SC, SC, T.XC[:], O.mult, ["XC"], ["ps5"], CAP, 1)
        vtt(T.XN[:], SC, XFP, O.add, ["XF" + p], ["XN", "ps5"], CAP, 1)
        tk("V", cost(CAP, SCA), ["XN", "AW" + p], ["XA"], lambda: V.tensor_copy(T.XA[:, 0:WE].indirect(AW15), T.XN[:]))

    for w in range(RO):
        wave(w)
    vts(T.YM[:], T.FX[:, 0:VA], 0.0, 2559.0 + OFF, O.is_equal, O.mult, ["FX"], ["YM"], VA)
    act(T.Y1[:], T.FX[:, 0:VA], F.Copy, ["FX"], ["Y1"], VA, bias=-float(OFF))
    vtt(T.YO[:], T.Y1[:], T.YM[:], O.add, ["Y1", "YM"], ["YO"], VA)
    tk("S", 0.1, ["YO"], ["yf"], lambda: SY.dma_start(T.yf[:], T.YO[:]), sem="oy", val=16)
    tk("S", 0.1, ["XA"], ["ya"], lambda: SY.dma_start(T.ya[:], T.XA[:, 0:VA]), sem="ox", val=16)
    return tasks, sent


LAT = {"V": 0.05, "A": 0.08, "P": 0.1, "G": 0.1, None: 0.0}
EPS = 0.06
BONUS = {}


def plan(tasks):
    n = len(tasks)
    succ = [[] for _ in range(n)]
    for i, t in enumerate(tasks):
        for d in t["deps"]:
            succ[d].append(i)
    lat = [LAT[t["q"]] if t["sem"] is None or t["q"] is None else 2.2 for t in tasks]
    prio = [0.0] * n
    for i in range(n - 1, -1, -1):
        prio[i] = tasks[i]["dur"] + lat[i] + max([prio[j] for j in succ[i]] + [0.0])
    prio = [p + BONUS.get(t["tag"], 0.0) for p, t in zip(prio, tasks)]
    left = [len(t["deps"]) for t in tasks]
    est, fin, free, order = [0.0] * n, [0.0] * n, {}, []
    ready = {}
    for i in range(n):
        if left[i] == 0:
            ready.setdefault(tasks[i]["q"], []).append(i)
    while len(order) < n:
        best = None
        for q, lst in ready.items():
            if not lst:
                continue
            f = free.get(q, 0.0) if q is not None else 0.0
            t0 = min(max(f, est[i]) for i in lst)
            c = max((i for i in lst if max(f, est[i]) <= t0 + EPS), key=lambda i: prio[i])
            if best is None or t0 < best[0]:
                best = (t0, q, c)
        t0, q, i = best
        ready[q].remove(i)
        fin[i] = (est[i] if q is None else max(t0, est[i])) + tasks[i]["dur"]
        if q is not None:
            free[q] = fin[i]
        order.append(i)
        for j in succ[i]:
            est[j] = max(est[j], fin[i] + lat[i])
            left[j] -= 1
            if left[j] == 0:
                ready.setdefault(tasks[j]["q"], []).append(j)
    return order, fin


def emit(g, T, tasks, order):
    queues = {"V": g.vector, "A": g.scalar, "P": g.tensor, "G": g, "S": g.sync}
    esem = {"V": "sV", "A": "sA", "P": "sP", "G": "sG"}
    cnt = {k: 0 for k in esem}
    known = {k: {} for k in queues}
    done, clock, final = [None] * len(tasks), [None] * len(tasks), {}
    for i in order:
        t = tasks[i]
        q = t["q"]
        if q is None:
            done[i] = (t["sem"], t["val"])
            clock[i] = {t["sem"]: t["val"]}
            final[t["sem"]] = t["val"]
            continue
        kn = known[q]
        need = [d for d, hard in t["deps"].items() if done[d] is not None and (hard or tasks[d]["q"] != q or tasks[d]["sem"] is not None)]
        need.sort(key=lambda d: -done[d][1])
        for d in need:
            s, v = done[d]
            if kn.get(s, 0) < v:
                queues[q].wait_ge(T.sem[s], v)
            for a, b in clock[d].items():
                if kn.get(a, 0) < b:
                    kn[a] = b
        x = t["fn"]()
        if t["sem"] == "none":
            continue
        if t["sem"] is not None:
            x.then_inc(T.sem[t["sem"]], 16)
            done[i] = (t["sem"], 16)
        else:
            cnt[q] += 1
            x.then_inc(T.sem[esem[q]], 1)
            done[i] = (esem[q], cnt[q])
        clock[i] = dict(kn)
        clock[i][done[i][0]] = done[i][1]
        final[done[i][0]] = max(final.get(done[i][0], 0), done[i][1])
    return final


def rank_program(g, core, T, topo):
    msgs = messages(topo, T.cores)
    if T.rank_of(core) is None:
        relay_program(g, core, T, topo, msgs)
        return
    tasks, sent = build(g, core, T, topo, msgs)
    order, _fin = plan(tasks)
    final = emit(g, T, tasks, order)
    for s, v in final.items():
        g.wait_ge(T.sem[s], v)
    g.wait_ge(T.sem["ls"], sent[0])
